import numpy as np
import ml_dtypes


def mxq(x, axis, fmt="e4m3"):
    dtype, down = {"e4m3": (ml_dtypes.float8_e4m3fn, 7), "e5m2": (ml_dtypes.float8_e5m2, 14)}[fmt]
    v = np.moveaxis(np.asarray(x, np.float32).astype(ml_dtypes.bfloat16).astype(np.float64), axis, -1)
    blocks = v.reshape(v.shape[:-1] + (-1, 32))
    amax = np.abs(blocks).max(-1, keepdims=True)
    byte = np.maximum(np.where(amax > 0, np.frexp(amax)[1] - 1 + 127, 0) - down, 1)
    scale = np.exp2(byte - 127.0)
    codes = (blocks / scale).astype(np.float32).astype(dtype).astype(np.float64)
    return np.moveaxis((codes * scale).reshape(v.shape), -1, axis)


WIDE = False


def mx_kscale(k):
    if not WIDE:
        return np.ones(k)
    levels = np.array([10, -10, 5, -5, 0])
    if k % 512:
        return np.exp2(np.random.permutation(np.resize(levels, k // 32))).repeat(32)
    a = np.empty((k // 512, 16))
    for p in range(k // 512):
        a[p, :8] = np.random.permutation(np.resize(levels, 8))
        for g in range(8):
            far = levels[np.abs(levels - a[p, g]) >= 10]
            a[p, g + 8] = far[np.random.randint(len(far))]
    return np.exp2(a.ravel()).repeat(32)


BF16 = ml_dtypes.bfloat16


def bf(x):
    return np.asarray(x, np.float32).astype(BF16)


def f64(x):
    return np.asarray(x).astype(np.float64)


B, R, CE, T = 4, 16, 32, 3
W = R
SG = R
C = SG * CE
K = R * CE
N = B * R * W


def permute_in(x):
    x5 = x.reshape(B, R, W, SG, CE)
    p0 = np.transpose(x5, (0, 2, 3, 1, 4)).reshape(N, K)
    p1 = np.transpose(x5, (0, 1, 3, 2, 4)).reshape(N, K)
    p2 = x.reshape(N, K)
    return p0, p1, p2


def permute_back(t0, t1, t2):
    y0 = np.transpose(t0.reshape(B, W, SG, R, CE), (0, 3, 1, 2, 4)).reshape(B, R, W, C)
    y1 = np.transpose(t1.reshape(B, R, SG, W, CE), (0, 1, 3, 2, 4)).reshape(B, R, W, C)
    y2 = t2.reshape(B, R, W, C)
    return y0, y1, y2


def softmax(v, axis):
    e = np.exp(v - v.max(axis=axis, keepdims=True))
    return e / e.sum(axis=axis, keepdims=True)


def draw0():
    s = np.stack([mx_kscale(K) for _ in range(T)])
    t = mx_kscale(C)
    return {
        "x": bf(np.random.standard_normal((B, R, W, C))),
        "g": bf((1.0 + 0.1 * np.random.standard_normal((T, K))) * s),
        "w": bf(np.random.standard_normal((T, K, K)) / np.sqrt(K) / s[:, :, None]),
        "b": bf(0.5 * np.random.standard_normal((T, K))),
        "ka": bf(2.0 * np.random.standard_normal((T, C))),
        "gp": bf((1.0 + 0.1 * np.random.standard_normal(C)) * t),
        "wp": bf(1.5 * np.random.standard_normal((C, C)) / np.sqrt(C) / t[:, None]),
    }


def core(x, g, w, b, ka, gp, wp):
    x, g, w, b, ka, gp, wp = f64(x), f64(g), f64(w), f64(b), f64(ka), f64(gp), f64(wp)
    p0, p1, p2 = permute_in(x)

    u0 = p0 * g[0]
    u1 = p1 * g[1]
    u2 = p2 * g[2]

    t0 = (mxq(u0, 1, "e4m3") @ mxq(w[0], 0, "e4m3")) + b[0]
    t1 = (mxq(u1, 1, "e4m3") @ mxq(w[1], 0, "e4m3")) + b[1]
    t2 = (mxq(u2, 1, "e4m3") @ mxq(w[2], 0, "e4m3")) + b[2]

    y0, y1, y2 = permute_back(t0, t1, t2)

    pool = np.mean(y0 + y1 + y2, axis=(1, 2))

    a = softmax(ka[None, :, :] * pool[:, None, :], 1)

    a0 = a[:, 0][:, None, None, :]
    a1 = a[:, 1][:, None, None, :]
    a2 = a[:, 2][:, None, None, :]
    f = (a0 * y0 + a1 * y1 + a2 * y2) * gp

    return mxq(f, 3, "e4m3") @ mxq(wp, 0, "e4m3")


def e4m3fn_bytes(y):
    return np.clip(np.asarray(y, np.float64), -448.0, 448.0).astype(np.float32).astype(ml_dtypes.float8_e4m3fn).view(np.uint8)


def e4m3fn_values(b):
    return np.asarray(b, np.uint8).view(ml_dtypes.float8_e4m3fn).astype(np.float64)


def setup_inputs():
    d = draw0()
    x0 = np.asarray(d['wp']).astype(np.float64)
    s = (np.max(np.abs(x0), axis=(1,), keepdims=True) / 448.0).astype(np.float32)
    out = {}
    for k, v in d.items():
        if k == 'wp':
            out['wp_bytes'] = e4m3fn_bytes(x0 / s.astype(np.float64))
            out['wp_scale'] = s
        else:
            out[k] = v
    return out


def reference(x, g, w, b, ka, gp, wp_bytes, wp_scale):
    return core(x, g, w, b, ka, gp, e4m3fn_values(wp_bytes) * wp_scale.astype(np.float64))

@@ -1,0 +1,612 @@
+from contextlib import ExitStack
+
+import concourse.mybir as mybir
+from concourse.masks import make_identity
+
+F32 = mybir.dt.float32
+BF16 = mybir.dt.bfloat16
+U32 = mybir.dt.uint32
+I32 = mybir.dt.int32
+U8 = mybir.dt.uint8
+E4M3 = mybir.dt.float8_e4m3fn
+FP8X4 = mybir.dt.float8_e4m3fn_x4
+ADD = mybir.AluOpType.add
+MULT = mybir.AluOpType.mult
+MAX = mybir.AluOpType.max
+SUB = mybir.AluOpType.subtract
+AX = mybir.AxisListType.X
+ACT = mybir.ActivationFunctionType
+
+P = 128
+FLOPS = 4 * 2 * 1024 * 512 * 512
+
+
+def tile_visionpermutatorsegmentmixing_kernel(tc, x, g, w, b, ka, gp, wp_bytes, wp_scale, out):
+    nc = tc.nc
+    with ExitStack() as ctx:
+        keep = ctx.enter_context(tc.tile_pool(name="keep", bufs=1))
+        work = ctx.enter_context(tc.tile_pool(name="work", bufs=4))
+        psum = ctx.enter_context(tc.psum_pool(name="psum", bufs=2))
+
+        def sb(shape, dtype, name):
+            return keep.tile(shape, dtype, name=name, align_bytes=64)
+
+        def bank(kind, bufs, name, dtype=F32, width=512):
+            return psum.tile([P, width], dtype, name=name, tag=kind, bufs=bufs)
+
+        def tr_bank(name, dtype=F32, width=512):
+            return bank("tr", 2, name, dtype, width)
+
+        def ym_bank(name, dtype=F32, width=512):
+            return bank("ym", 2, name, dtype, width)
+
+        def mm_bank(name):
+            return bank("mm", 2, name)
+
+        def pa_bank(name):
+            return bank("pa", 2, name)
+
+        pad_codes = sb([P, 16, 224], U32, "pad_codes")
+        pad_scales = sb([P, 4, 16, P], U8, "pad_scales")
+        w_codes = [sb([P, 512], U32, "w_codes%d" % m) for m in range(4)]
+        w_scales = [sb([P, 512], U8, "w_scales%d" % m) for m in range(4)]
+
+        gains = sb([P, 3, 512], BF16, "gains")
+        nc.sync.dma_start(
+            out=gains[:].rearrange("p m k -> p (m k)"), in_=g.rearrange("m k -> (m k)").partition_broadcast(P)
+        )
+        small = sb([P, P], BF16, "small")
+        nc.vector.memset(small[:], 0.0)
+        nc.scalar.dma_start(
+            out=small[0:32, :].rearrange("r (q e) -> r q e", q=4),
+            in_=b[0:2, :].rearrange("m (i e) -> (m i) e", e=32).unsqueeze(1).to_broadcast([32, 4, 32]),
+        )
+        nc.scalar.dma_start(out=small[32:36, :], in_=b[2:3, :].rearrange("o (c x) -> (o c) x", x=P))
+        nc.scalar.dma_start(out=small[36:48, :], in_=ka.rearrange("m (c x) -> (m c) x", x=P))
+        nc.scalar.dma_start(out=small[48:52, :], in_=gp.rearrange("(c x) -> c x", x=P))
+
+        x_tok = x.rearrange("n i j c -> (n i j) c").rearrange("(t p) c -> p t c", p=P)
+        x2 = sb([P, 8, 512], BF16, "x2")
+        x0 = sb([P, 16, 256], BF16, "x0")
+        x1 = sb([P, 16, 256], BF16, "x1")
+        w_raw = [sb([P, 4, 512], BF16, "w_raw%d" % m) for m in range(3)]
+
+        def load_x2(h):
+            nc.sync.dma_start(out=x2[:, 4 * h : 4 * h + 4, :], in_=x_tok[:, 4 * h : 4 * h + 4, :])
+
+        def load_w(m):
+            nc.sync.dma_start(out=w_raw[m][:], in_=w[m].rearrange("(p j) n -> p j n", j=4))
+
+        load_x2(0)
+        for h in range(2):
+            nc.sync.dma_start(
+                out=x1[h : P : 2, :, :],
+                in_=x[:, :, :, 256 * h : 256 * h + 256].rearrange("n i j c -> (n i) j c"),
+            )
+        load_w(1)
+        load_x2(1)
+        for n in range(4):
+            nc.sync.dma_start(out=x0[n : P : 4, :, :], in_=x[n].rearrange("i j (h c) -> (j h) i c", h=2))
+        load_w(0)
+        load_w(2)
+        wp_codes = sb([P, 4, 512], U8, "wp_codes")
+        nc.sync.dma_start(out=wp_codes[:], in_=wp_bytes.rearrange("(p j) n -> p j n", j=4))
+        wp_s = sb([P, 4], F32, "wp_s")
+        nc.sync.dma_start(out=wp_s[:], in_=wp_scale.rearrange("(p j) o -> p (j o)", j=4))
+
+        ident = sb([P, P], F32, "ident")
+        make_identity(nc, ident[:])
+        nc.gpsimd.memset(w_scales[1][:].bitcast(I32), 0)
+        nc.gpsimd.memset(pad_codes[:], 0)
+        nc.gpsimd.memset(pad_scales[:].bitcast(I32), 0)
+        ident_bf = sb([P, P], BF16, "ident_bf")
+        nc.vector.tensor_copy(out=ident_bf[:], in_=ident[:])
+        perm0 = sb([P, P], F32, "perm0")
+        nc.vector.tensor_copy(
+            out=perm0[:].rearrange("p (h n y) -> p h n y", h=2, n=4),
+            in_=ident[:].rearrange("p (y h n) -> p h n y", h=2, n=4),
+        )
+        perm1 = sb([P, P], F32, "perm1")
+        nc.vector.tensor_copy(
+            out=perm1[:].rearrange("p (h z) -> p h z", h=2),
+            in_=ident[:].rearrange("p (z h) -> p h z", h=2),
+        )
+        e_sum = sb([P, 32], F32, "e_sum")
+        nc.vector.tensor_reduce(out=e_sum[:], in_=ident[:].rearrange("p (a e) -> p e a", e=32), axis=AX, op=ADD)
+        e_sel = sb([P, P], F32, "e_sel")
+        nc.vector.tensor_copy(
+            out=e_sel[:].rearrange("p (q e) -> p q e", q=4), in_=e_sum[:].unsqueeze(1).to_broadcast([P, 4, 32])
+        )
+        q_mask = sb([P, 4], F32, "q_mask")
+        nc.vector.tensor_reduce(out=q_mask[:], in_=ident[:].rearrange("p (q e) -> p q e", q=4), axis=AX, op=ADD)
+        nc.vector.tensor_scalar(out=q_mask[:], in0=q_mask[:], scalar1=1.0 / 256.0, scalar2=None, op0=MULT)
+        l_mask = sb([P, 2], F32, "l_mask")
+        nc.vector.tensor_reduce(out=l_mask[:], in_=ident[:].rearrange("p (l y) -> p l y", l=2), axis=AX, op=ADD)
+        nc.vector.tensor_scalar(out=l_mask[:], in0=l_mask[:], scalar1=1.0 / 256.0, scalar2=None, op0=MULT)
+        warm = sb([P, 1], F32, "warm")
+        nc.scalar.activation(out=warm[:], in_=e_sum[:, 0:1], func=ACT.Exp)
+
+        sm_ps = tr_bank("sm_ps", BF16)
+        nc.tensor.transpose(sm_ps[:, 0:P], small[:], ident_bf[:])
+        vec = sb([P, 52], F32, "vec")
+        nc.scalar.copy(out=vec[:], in_=sm_ps[:, 0:52])
+
+        grouped = [sb([P, 4096], BF16, "grouped%d" % m) for m in range(3)]
+        u_codes = [sb([P, 1024], U32, "u_codes%d" % m) for m in range(3)]
+        u_scales = [sb([P, 1024], U8, "u_scales%d" % m) for m in range(3)]
+        u = [keep.tile([P, 8, 512], BF16, name="u%d" % m, tag="u%d" % m, align_bytes=64) for m in range(2)] + [x2]
+        xs = [x0, x1, x2]
+        perms = [perm0, perm1, ident]
+        t_banks = {}
+        full = slice(0, 512)
+
+        def gain(m, q):
+            if m == 2:
+                nc.vector.tensor_tensor(
+                    out=u[2][:, 2 * q : 2 * q + 2, :],
+                    in0=x2[:, 2 * q : 2 * q + 2, :],
+                    in1=gains[:, 2, :].unsqueeze(1).to_broadcast([P, 2, 512]),
+                    op=MULT,
+                )
+            else:
+                nc.vector.tensor_tensor(
+                    out=u[m][:, q:8:4, :].rearrange("p s (z e) -> p s z e", e=32),
+                    in0=xs[m][:].rearrange("p z (s e) -> p s z e", e=32)[:, q:8:4, :, :],
+                    in1=gains[:, m, :].rearrange("p (z e) -> p z e", e=32).unsqueeze(1).to_broadcast([P, 2, 16, 32]),
+                    op=MULT,
+                )
+
+        def turn(m, q):
+            ps = tr_bank("t%d_%d" % (m, q))
+            t_banks[m, q] = ps
+            view = ps[:].rearrange("p (u t c) -> p u t c", t=2, u=2)
+            words = u[m][:].bitcast(F32)
+            for t in range(2):
+                for v in range(2):
+                    row = 2 * q + t if m == 2 else q + 4 * t
+                    nc.tensor.transpose(view[:, v, t, :], words[:, row, v::2], perms[m][:])
+
+        def evac(m, q):
+            ps = t_banks[m, q]
+            words = grouped[m][:].bitcast(F32)
+            if m == 1:
+                nc.scalar.copy(
+                    out=words[:, 512 * q : 512 * q + 512].rearrange("p (c u) -> p c u", u=2),
+                    in_=ps[:].rearrange("p (u c) -> p c u", u=2),
+                )
+            elif m == 0:
+                nc.scalar.copy(
+                    out=words.rearrange("p (k q r u) -> p k q r u", q=4, r=32, u=2)[:, :, q, :, :],
+                    in_=ps[:].rearrange("p (u k r) -> p k r u", u=2, r=32),
+                )
+            else:
+                nc.scalar.copy(
+                    out=words.rearrange("p (n x l y u) -> p n l x y u", n=2, x=4, l=2, u=2)[:, q // 2, q % 2, :, :, :],
+                    in_=ps[:].rearrange("p (u x y) -> p x y u", u=2, x=4),
+                )
+
+        def quant_u(m, half):
+            cols = slice(512 * half, 512 * half + 512)
+            nc.vector.quantize_mx(
+                out=u_codes[m][:, cols].bitcast(FP8X4),
+                scales=u_scales[m][:, cols],
+                in_=grouped[m][:, 2048 * half : 2048 * half + 2048],
+            )
+
+        w_groups = [sb([P, 512, 4], BF16, "w_grouped%d" % m) for m in range(3)]
+        w_groups.append(w_groups[0])
+
+        def w_inter(m, eng, h, parts=2):
+            n = 512 // parts
+            src = (w_raw + [wp_w])[m]
+            dst = w_groups[m][:, n * h : n * h + n, :]
+            src = src[:, :, n * h : n * h + n].rearrange("p j n -> p n j")
+            if eng == "s":
+                nc.scalar.copy(out=dst, in_=src)
+            elif eng == "v":
+                nc.vector.tensor_copy(out=dst, in_=src)
+            else:
+                nc.gpsimd.tensor_scalar(out=dst, in0=src, scalar1=1.0, scalar2=0.0, op0=MULT, op1=ADD)
+
+        def w_quant(m):
+            nc.vector.quantize_mx(
+                out=w_codes[m][:].bitcast(FP8X4),
+                scales=w_scales[m][:],
+                in_=w_groups[m][:].rearrange("p n j -> p (n j)"),
+            )
+
+        def mx_raw(o, lc, ls, rc, rs, start, stop):
+            nc.tensor.matmul_mx(
+                out=o, lhsT=lc.bitcast(FP8X4), lhsT_scale=ls, rhs=rc.bitcast(FP8X4), rhs_scale=rs, start=start, stop=stop
+            )
+
+        def mx(o, m, lcols, rcols, w_stationary, start=True, stop=True):
+            u_c, u_s = u_codes[m], u_scales[m]
+            w_c, w_s = w_codes[m], w_scales[m]
+            lc, ls, rc, rs = (w_c, w_s, u_c, u_s) if w_stationary else (u_c, u_s, w_c, w_s)
+            mx_raw(o, lc[:, lcols], ls[:, lcols], rc[:, rcols], rs[:, rcols], start, stop)
+
+        red = [sb([P, 8, 4, 2], F32, "red%d" % m) for m in range(2)]
+
+        def pool_mm(m, half):
+            ps = pa_bank("pa%d_%d" % (m, half))
+            t_banks["pool", m, half] = ps
+            for z in range(4):
+                mx(ps[:], m, slice(128 * z, 128 * z + 128), slice(512 * half, 512 * half + 512), True, z == 0, z == 3)
+
+        def pool_red(m, half):
+            ps = t_banks["pool", m, half]
+            if m == 1:
+                dst = red[1][:].rearrange("p k q l -> p q k l")[:, 2 * half : 2 * half + 2, :, :]
+                src = ps[:].rearrange("p (q k l y) -> p q k l y", q=2, k=8, l=2)
+            else:
+                dst = red[0][:, 4 * half : 4 * half + 4, :, :]
+                src = ps[:].rearrange("p (k q l y) -> p k q l y", k=4, q=4, l=2)
+            nc.vector.tensor_reduce(out=dst, in_=src, axis=AX, op=ADD)
+
+        pb_sb = sb([P, 2, 512], F32, "pb_sb")
+
+        def pool2_mm(n):
+            ps = pa_bank("pb%d" % n)
+            for t in range(4):
+                c0 = 512 * n + 128 * t
+                mx(ps[:], 2, slice(c0, c0 + 128), full, False, t == 0, t == 3)
+            t_banks["pb", n] = ps
+
+        def pool2_out(n):
+            nc.scalar.copy(out=pb_sb[:, n, :], in_=t_banks["pb", n][:])
+
+        def pad_moves():
+            nc.vector.tensor_copy(
+                out=pad_codes[:, :, 96:128].bitcast(I32),
+                in_=w_codes[1][:].rearrange("p (z e) -> p z e", e=32).bitcast(I32),
+            )
+            for q in range(4):
+                nc.vector.tensor_copy(
+                    out=pad_scales[:].rearrange("p q z x -> p (q z x)").bitcast(I32).rearrange(
+                        "p (q z x) -> p q z x", q=4, z=16
+                    )[:, q, :, 8 * q : 8 * q + 8],
+                    in_=w_scales[1][:].bitcast(I32).rearrange("p (z x) -> p z x", x=8),
+                )
+
+        y0 = sb([P, 8, 16, 32], F32, "y0")
+        y1 = sb([P, 16, 16, 16], F32, "y1")
+
+        def y1_mm(pair):
+            ps = ym_bank("ym%d" % pair)
+            t_banks["y1", pair] = ps
+            for d in range(2):
+                z = 2 * pair + d
+                for q in range(4):
+                    mx_raw(
+                        ps[:, 256 * d : 256 * d + 256],
+                        pad_codes[:, z, 96 - 32 * q : 224 - 32 * q],
+                        pad_scales[:, q, z, :],
+                        u_codes[1][:, 256 * q : 256 * q + 256],
+                        u_scales[1][:, 256 * q : 256 * q + 256],
+                        q == 0,
+                        q == 3,
+                    )
+
+        def y1_out(pair):
+            ps = t_banks["y1", pair]
+            for d in range(2):
+                z = 2 * pair + d
+                nc.scalar.activation(
+                    out=y1[:, z, :, :].rearrange("p k i -> p (k i)"),
+                    in_=ps[:, 256 * d : 256 * d + 256],
+                    func=ACT.Identity,
+                    bias=vec[:, 16 + z : 17 + z],
+                )
+
+        def y0_mm(k):
+            ps = mm_bank("y0_%d" % k)
+            t_banks["y0", k] = ps
+            mx(ps[:], 0, slice(128 * k, 128 * k + 128), full, False)
+
+        def y0_out(k):
+            nc.vector.transpose(out=y0[:, k, :, :].rearrange("p z r -> p (z r)"), in_=t_banks["y0", k][:])
+
+        def y0_bias(z):
+            nc.vector.tensor_scalar(
+                out=y0[:, :, z, :], in0=y0[:, :, z, :], scalar1=vec[:, z : z + 1], scalar2=None, op0=ADD
+            )
+
+        b_mean = sb([P, 1], F32, "b_mean")
+        b_pool = sb([P, 4], F32, "b_pool")
+
+        def bias_mean():
+            nc.vector.tensor_reduce(out=b_mean[:], in_=vec[:, 0:32], axis=AX, op=ADD)
+            nc.vector.scalar_tensor_tensor(
+                out=b_pool[:],
+                in0=b_mean[:].to_broadcast([P, 4]),
+                scalar=1.0 / 16.0,
+                in1=vec[:, 32:36],
+                op0=MULT,
+                op1=ADD,
+            )
+
+
+        wp_w = sb([P, 4, 512], BF16, "wp_w")
+
+        def wp_widen(j):
+            nc.scalar.activation(
+                out=wp_w[:, j, :], in_=wp_codes[:, j, :].bitcast(E4M3), func=ACT.Copy, scale=wp_s[:, j : j + 1]
+            )
+
+        amp = sb([P, 3, 16], F32, "amp")
+        a2b2 = sb([P, 4, 4], F32, "a2b2")
+
+        def softmax():
+            sel_ps = tr_bank("sel_ps")
+            for m in range(2):
+                nc.tensor.matmul(
+                    sel_ps[:, 0:64],
+                    lhsT=e_sel[:],
+                    rhs=red[m][:].rearrange("p k q l -> p (k q l)"),
+                    start=(m == 0),
+                    stop=(m == 1),
+                )
+            picked = sb([P, 8, 4, 2], F32, "picked")
+            nc.vector.tensor_tensor(
+                out=picked[:],
+                in0=sel_ps[:, 0:64].rearrange("p (k q l) -> p k q l", k=8, q=4),
+                in1=q_mask[:].unsqueeze(1).unsqueeze(3).to_broadcast([P, 8, 4, 2]),
+                op=MULT,
+            )
+            pool01 = sb([P, 2, 2, 2, 2], F32, "pool01")
+            nc.vector.tensor_reduce(
+                out=pool01[:].rearrange("p f h n l -> p (f h n) l"),
+                in_=picked[:].rearrange("p k q l -> p k l q"),
+                axis=AX,
+                op=ADD,
+            )
+            p2_ps = tr_bank("p2_ps")
+            for c in range(4):
+                for n in range(2):
+                    k = 4 * c + 2 * n
+                    nc.tensor.matmul(
+                        p2_ps[:, k : k + 2],
+                        lhsT=pb_sb[:, n, 128 * c : 128 * c + 128],
+                        rhs=l_mask[:],
+                        start=True,
+                        stop=True,
+                    )
+            pool_a = sb([P, 4, 4], F32, "pool_a")
+            nc.vector.tensor_tensor(
+                out=pool_a[:],
+                in0=p2_ps[:, 0:16].rearrange("p (c n) -> p c n", c=4),
+                in1=b_pool[:].unsqueeze(2).to_broadcast([P, 4, 4]),
+                op=ADD,
+            )
+            pool = sb([P, 4, 4], F32, "pool")
+            nc.vector.tensor_tensor(
+                out=pool[:].rearrange("p (h f) n -> p h f n", h=2),
+                in0=pool_a[:].rearrange("p (h f) n -> p h f n", h=2),
+                in1=pool01[:].rearrange("p f h n l -> p h f (n l)"),
+                op=ADD,
+            )
+            logit = sb([P, 3, 16], F32, "logit")
+            nc.vector.tensor_tensor(
+                out=logit[:].rearrange("p m (c n) -> p m c n", c=4),
+                in0=pool[:].unsqueeze(1).to_broadcast([P, 3, 4, 4]),
+                in1=vec[:, 36:48].rearrange("p (m c) -> p m c", m=3).unsqueeze(3).to_broadcast([P, 3, 4, 4]),
+                op=MULT,
+            )
+            l_max = sb([P, 16], F32, "l_max")
+            nc.vector.tensor_reduce(out=l_max[:], in_=logit[:].rearrange("p m k -> p k m"), axis=AX, op=MAX)
+            shifted = sb([P, 3, 16], F32, "shifted")
+            nc.vector.tensor_tensor(
+                out=shifted[:], in0=logit[:], in1=l_max[:].unsqueeze(1).to_broadcast([P, 3, 16]), op=SUB
+            )
+            expo = sb([P, 3, 16], F32, "expo")
+            nc.scalar.activation(out=expo[:], in_=shifted[:], func=ACT.Exp)
+            e_tot = sb([P, 16], F32, "e_tot")
+            nc.vector.tensor_reduce(out=e_tot[:], in_=expo[:].rearrange("p m k -> p k m"), axis=AX, op=ADD)
+            e_inv = sb([P, 16], F32, "e_inv")
+            nc.vector.reciprocal(out=e_inv[:], in_=e_tot[:])
+            e_gp = sb([P, 4, 4], F32, "e_gp")
+            nc.vector.tensor_tensor(
+                out=e_gp[:],
+                in0=e_inv[:].rearrange("p (c n) -> p c n", c=4),
+                in1=vec[:, 48:52].unsqueeze(2).to_broadcast([P, 4, 4]),
+                op=MULT,
+            )
+            nc.vector.tensor_tensor(
+                out=amp[:],
+                in0=expo[:],
+                in1=e_gp[:].rearrange("p c n -> p (c n)").unsqueeze(1).to_broadcast([P, 3, 16]),
+                op=MULT,
+            )
+            nc.vector.tensor_tensor(
+                out=a2b2[:],
+                in0=amp[:, 2, :].rearrange("p (c n) -> p c n", c=4),
+                in1=vec[:, 32:36].unsqueeze(2).to_broadcast([P, 4, 4]),
+                op=MULT,
+            )
+
+        f_sb = keep.tile([P, 4, 4, 256], BF16, name="f_sb", tag="u0", align_bytes=64)
+
+        def y2_mm(nh, c):
+            ps = mm_bank("y2_%d_%d" % (nh, c))
+            t_banks["y2", nh, c] = ps
+            mx(ps[:], 2, slice(128 * c, 128 * c + 128), slice(512 * nh, 512 * nh + 512), True)
+
+        v1_tiles = {}
+
+        def combine1(nh, c):
+            view = t_banks["y2", nh, c][:].rearrange("p (x l y) -> p l x y", x=4, l=2)
+            for l in range(2):
+                k = 4 * c + 2 * nh + l
+                t = work.tile([P, 16, 16], F32, name="v1", bufs=16)
+                v1_tiles[c, 2 * nh + l] = t
+                nc.scalar.activation(
+                    out=t[:].rearrange("p i j -> p (i j)").rearrange("p (x y) -> p x y", x=4),
+                    in_=view[:, l, :, :],
+                    func=ACT.Identity,
+                    scale=amp[:, 2, k : k + 1],
+                    bias=a2b2[:, c, 2 * nh + l : 2 * nh + l + 1],
+                )
+
+        def combine23(n, pair):
+            nh, l = n // 2, n % 2
+            v2 = []
+            for c in (2 * pair, 2 * pair + 1):
+                f, h = c % 2, c // 2
+                k = 4 * c + n
+                t = work.tile([P, 16, 16], F32, name="v2")
+                v2.append(t)
+                nc.vector.scalar_tensor_tensor(
+                    out=t[:],
+                    in0=y0[:, 4 * f + 2 * h + nh, :, 16 * l : 16 * l + 16],
+                    scalar=amp[:, 0, k : k + 1],
+                    in1=v1_tiles[c, n][:],
+                    op0=MULT,
+                    op1=ADD,
+                )
+            for c in (2 * pair, 2 * pair + 1):
+                f, h = c % 2, c // 2
+                k = 4 * c + n
+                nc.vector.scalar_tensor_tensor(
+                    out=f_sb[:, c, n, :].rearrange("p (i j) -> p i j", i=16),
+                    in0=y1[:, :, 8 * f + 4 * h + n, :].rearrange("p j i -> p i j"),
+                    scalar=amp[:, 1, k : k + 1],
+                    in1=v2[c % 2][:],
+                    op0=MULT,
+                    op1=ADD,
+                )
+
+        f_tiles = {}
+
+        def f_turn_a(n, h):
+            ps = ym_bank("ta%d_%d" % (n, h), BF16, 512)
+            for c in range(4):
+                nc.tensor.transpose(
+                    ps[:, 128 * c : 128 * c + 128], f_sb[:, c, n, 128 * h : 128 * h + 128], ident_bf[:]
+                )
+            ft = work.tile([P, 512], BF16, name="ft")
+            nc.scalar.copy(out=ft[:], in_=ps[:])
+            f_tiles["a", n, h] = ft
+
+        def f_turn_b(n, h):
+            ps = tr_bank("tb%d_%d" % (n, h), F32, 256)
+            words = f_tiles["a", n, h][:].bitcast(F32)
+            for v in range(2):
+                nc.tensor.transpose(ps[:, 128 * v : 128 * v + 128], words[:, v::2], ident[:])
+            fg = work.tile([P, 512], BF16, name="fg", align_bytes=64)
+            nc.scalar.copy(
+                out=fg[:].bitcast(F32).rearrange("p (c u) -> p c u", u=2), in_=ps[:].rearrange("p (u c) -> p c u", u=2)
+            )
+            f_tiles[n, h] = fg
+
+        def f_project(n, h):
+            f_codes = work.tile([P, 128], U32, name="f_codes", align_bytes=64)
+            f_scales = work.tile([P, 128], U8, name="f_scales", align_bytes=64)
+            nc.vector.quantize_mx(out=f_codes[:].bitcast(FP8X4), scales=f_scales[:], in_=f_tiles[n, h][:])
+            po = pa_bank("po%d_%d" % (n, h))
+            mx_raw(po[:], f_codes[:], f_scales[:], w_codes[3][:], w_scales[3][:], True, True)
+            res = work.tile([P, 512], F32, name="res", bufs=4)
+            nc.scalar.copy(out=res[:], in_=po[:])
+            nc.sync.dma_start(out=out[n].rearrange("i j c -> (i j) c")[128 * h : 128 * h + 128, :], in_=res[:])
+
+        with tc.manual_schedule():
+            for q in range(2):
+                gain(2, q)
+                turn(2, q)
+                evac(2, q)
+            for q in range(4):
+                gain(1, q)
+                turn(1, q)
+                evac(1, q)
+            w_inter(1, "v", 1)
+            w_inter(1, "s", 0)
+            for q in range(2, 4):
+                gain(2, q)
+                turn(2, q)
+                evac(2, q)
+            quant_u(1, 0)
+            quant_u(1, 1)
+            w_quant(1)
+            pad_moves()
+            pool_mm(1, 0)
+            gain(0, 0)
+            turn(0, 0)
+            evac(0, 0)
+            gain(0, 1)
+            turn(0, 1)
+            evac(0, 1)
+            pool_mm(1, 1)
+            gain(0, 2)
+            turn(0, 2)
+            evac(0, 2)
+            gain(0, 3)
+            turn(0, 3)
+            evac(0, 3)
+            w_inter(0, "s", 0)
+            w_inter(2, "g", 0)
+            w_inter(2, "g", 1)
+            quant_u(2, 0)
+            quant_u(2, 1)
+            pool_red(1, 0)
+            pool_red(1, 1)
+            w_inter(0, "v", 1)
+            for k in range(3):
+                y1_mm(k)
+                y1_out(k)
+            quant_u(0, 0)
+            quant_u(0, 1)
+            w_quant(2)
+            w_quant(0)
+            pool2_mm(0)
+            pool2_out(0)
+            y0_mm(0)
+            y0_mm(1)
+            pool2_mm(1)
+            pool2_out(1)
+            for j in range(4):
+                wp_widen(j)
+            w_inter(3, "g", 0)
+            w_inter(3, "g", 1)
+            bias_mean()
+            y0_out(0)
+            y0_out(1)
+            for k in range(2, 4):
+                y0_mm(k)
+                y0_out(k)
+            pool_mm(0, 0)
+            for k in range(4, 6):
+                y0_mm(k)
+                y0_out(k)
+            pool_mm(0, 1)
+            pool_red(0, 0)
+            for k in range(6, 8):
+                y0_mm(k)
+                y0_out(k)
+            pool_red(0, 1)
+            y1_mm(3)
+            y1_out(3)
+            softmax()
+            for z in range(16):
+                y0_bias(z)
+            for k in range(4, 8):
+                y1_mm(k)
+                y1_out(k)
+                y2_mm(0, k - 4)
+                combine1(0, k - 4)
+            for c in range(4):
+                y2_mm(1, c)
+                combine1(1, c)
+            for n in range(4):
+                for pair in range(2):
+                    combine23(n, pair)
+                    if n >= 2:
+                        f_project(n - 2, pair)
+                if n == 1:
+                    w_quant(3)
+                for h in range(2):
+                    f_turn_a(n, h)
+                for h in range(2):
+                    f_turn_b(n, h)
+            for n in range(2, 4):
+                for h in range(2):
+                    f_project(n, h)

@@ -31,39 +31,27 @@ def tile_visionpermutatorsegmentmixing_kernel(tc, x, g, w, b, ka, gp, wp_bytes, 
         def sb(shape, dtype, name):
             return keep.tile(shape, dtype, name=name, align_bytes=64)
 
-        def bank(kind, bufs, name, dtype=F32, width=512):
-            return psum.tile([P, width], dtype, name=name, tag=kind, bufs=bufs)
+        def bank(name, dtype=F32, width=512):
+            return psum.tile([P, width], dtype, name=name, tag="bank", bufs=8)
 
-        def tr_bank(name, dtype=F32, width=512):
-            return bank("tr", 2, name, dtype, width)
+        tr_bank = ym_bank = mm_bank = pa_bank = bank
 
-        def ym_bank(name, dtype=F32, width=512):
-            return bank("ym", 2, name, dtype, width)
-
-        def mm_bank(name):
-            return bank("mm", 2, name)
-
-        def pa_bank(name):
-            return bank("pa", 2, name)
-
-        pad_codes = sb([P, 16, 224], U32, "pad_codes")
-        pad_scales = sb([P, 4, 16, P], U8, "pad_scales")
+        pad_codes = [sb([P, 96 + 16 * 128], U32, "pad_codes%d" % m) for m in range(2)]
+        pad_scales = [[sb([P, 768], U8, "pad_scales%d_%d" % (m, k)) for k in range(2)] for m in range(2)]
         w_codes = [sb([P, 512], U32, "w_codes%d" % m) for m in range(4)]
-        w_scales = [sb([P, 512], U8, "w_scales%d" % m) for m in range(4)]
+        w_scales = [
+            pad_scales[m][0][:, 128:640] if m < 2 else sb([P, 512], U8, "w_scales%d" % m)[:] for m in range(4)
+        ]
 
-        gains = sb([P, 3, 512], BF16, "gains")
-        nc.sync.dma_start(
-            out=gains[:].rearrange("p m k -> p (m k)"), in_=g.rearrange("m k -> (m k)").partition_broadcast(P)
-        )
+        ident = sb([P, P], F32, "ident")
+        make_identity(nc, ident[:])
+        g_row = sb([P, 3, 512], BF16, "g_row")
+        nc.vector.memset(g_row[:], 0.0)
+        nc.sync.dma_start(out=g_row[0:1, :, :], in_=g.rearrange("(o m) k -> o m k", o=1))
+        ones = sb([P, P], BF16, "ones")
+        nc.vector.memset(ones[:], 1.0)
         small = sb([P, P], BF16, "small")
         nc.vector.memset(small[:], 0.0)
-        nc.scalar.dma_start(
-            out=small[0:32, :].rearrange("r (q e) -> r q e", q=4),
-            in_=b[0:2, :].rearrange("m (i e) -> (m i) e", e=32).unsqueeze(1).to_broadcast([32, 4, 32]),
-        )
-        nc.scalar.dma_start(out=small[32:36, :], in_=b[2:3, :].rearrange("o (c x) -> (o c) x", x=P))
-        nc.scalar.dma_start(out=small[36:48, :], in_=ka.rearrange("m (c x) -> (m c) x", x=P))
-        nc.scalar.dma_start(out=small[48:52, :], in_=gp.rearrange("(c x) -> c x", x=P))
 
         x_tok = x.rearrange("n i j c -> (n i j) c").rearrange("(t p) c -> p t c", p=P)
         x2 = sb([P, 8, 512], BF16, "x2")
@@ -77,14 +65,23 @@ def tile_visionpermutatorsegmentmixing_kernel(tc, x, g, w, b, ka, gp, wp_bytes, 
         def load_w(m):
             nc.sync.dma_start(out=w_raw[m][:], in_=w[m].rearrange("(p j) n -> p j n", j=4))
 
-        load_x2(0)
-        for h in range(2):
-            nc.sync.dma_start(
-                out=x1[h : P : 2, :, :],
-                in_=x[:, :, :, 256 * h : 256 * h + 256].rearrange("n i j c -> (n i) j c"),
-            )
+        for part in range(2):
+            for h in range(2):
+                j = slice(8 * part, 8 * part + 8)
+                nc.sync.dma_start(
+                    out=x1[h : P : 2, j, :],
+                    in_=x[:, :, j, 256 * h : 256 * h + 256].rearrange("n i j c -> (n i) j c"),
+                )
         load_w(1)
+        load_x2(0)
         load_x2(1)
+        nc.sync.dma_start(
+            out=small[0:32, :].rearrange("r (q e) -> r q e", q=4),
+            in_=b[0:2, :].rearrange("m (i e) -> (m i) e", e=32).unsqueeze(1).to_broadcast([32, 4, 32]),
+        )
+        nc.sync.dma_start(out=small[32:36, :], in_=b[2:3, :].rearrange("o (c x) -> (o c) x", x=P))
+        nc.sync.dma_start(out=small[36:48, :], in_=ka.rearrange("m (c x) -> (m c) x", x=P))
+        nc.sync.dma_start(out=small[48:52, :], in_=gp.rearrange("(c x) -> c x", x=P))
         for n in range(4):
             nc.sync.dma_start(out=x0[n : P : 4, :, :], in_=x[n].rearrange("i j (h c) -> (j h) i c", h=2))
         load_w(0)
@@ -94,11 +91,6 @@ def tile_visionpermutatorsegmentmixing_kernel(tc, x, g, w, b, ka, gp, wp_bytes, 
         wp_s = sb([P, 4], F32, "wp_s")
         nc.sync.dma_start(out=wp_s[:], in_=wp_scale.rearrange("(p j) o -> p (j o)", j=4))
 
-        ident = sb([P, P], F32, "ident")
-        make_identity(nc, ident[:])
-        nc.gpsimd.memset(w_scales[1][:].bitcast(I32), 0)
-        nc.gpsimd.memset(pad_codes[:], 0)
-        nc.gpsimd.memset(pad_scales[:].bitcast(I32), 0)
         ident_bf = sb([P, P], BF16, "ident_bf")
         nc.vector.tensor_copy(out=ident_bf[:], in_=ident[:])
         perm0 = sb([P, P], F32, "perm0")
@@ -108,28 +100,39 @@ def tile_visionpermutatorsegmentmixing_kernel(tc, x, g, w, b, ka, gp, wp_bytes, 
         )
         perm1 = sb([P, P], F32, "perm1")
         nc.vector.tensor_copy(
-            out=perm1[:].rearrange("p (h z) -> p h z", h=2),
-            in_=ident[:].rearrange("p (z h) -> p h z", h=2),
+            out=perm1[:].rearrange("p (h y) -> p h y", h=2),
+            in_=ident[:].rearrange("p (y h) -> p h y", h=2),
         )
         e_sum = sb([P, 32], F32, "e_sum")
         nc.vector.tensor_reduce(out=e_sum[:], in_=ident[:].rearrange("p (a e) -> p e a", e=32), axis=AX, op=ADD)
-        e_sel = sb([P, P], F32, "e_sel")
-        nc.vector.tensor_copy(
-            out=e_sel[:].rearrange("p (q e) -> p q e", q=4), in_=e_sum[:].unsqueeze(1).to_broadcast([P, 4, 32])
-        )
-        q_mask = sb([P, 4], F32, "q_mask")
-        nc.vector.tensor_reduce(out=q_mask[:], in_=ident[:].rearrange("p (q e) -> p q e", q=4), axis=AX, op=ADD)
-        nc.vector.tensor_scalar(out=q_mask[:], in0=q_mask[:], scalar1=1.0 / 256.0, scalar2=None, op0=MULT)
+        e_sel = sb([P, 4, P], F32, "e_sel")
+        nc.vector.memset(e_sel[:], 0.0)
+        for q in range(4):
+            nc.vector.tensor_scalar(
+                out=e_sel[:, q, 32 * q : 32 * q + 32], in0=e_sum[:], scalar1=1.0 / 256.0, scalar2=None, op0=MULT
+            )
         l_mask = sb([P, 2], F32, "l_mask")
         nc.vector.tensor_reduce(out=l_mask[:], in_=ident[:].rearrange("p (l y) -> p l y", l=2), axis=AX, op=ADD)
         nc.vector.tensor_scalar(out=l_mask[:], in0=l_mask[:], scalar1=1.0 / 256.0, scalar2=None, op0=MULT)
+        for m in (1, 0):
+            for k in range(2):
+                nc.vector.memset(pad_scales[m][k][:].bitcast(I32), 0)
+            nc.gpsimd.memset(pad_codes[m][:].bitcast(I32), 0)
         warm = sb([P, 1], F32, "warm")
         nc.scalar.activation(out=warm[:], in_=e_sum[:, 0:1], func=ACT.Exp)
 
-        sm_ps = tr_bank("sm_ps", BF16)
-        nc.tensor.transpose(sm_ps[:, 0:P], small[:], ident_bf[:])
+        gains = sb([P, 3, 512], BF16, "gains")
+        for m in (1, 2, 0):
+            g_ps = tr_bank("g_ps%d" % m)
+            nc.tensor.matmul(g_ps[:], lhsT=ones[:], rhs=g_row[:, m, :], start=True, stop=True)
+            nc.scalar.copy(out=gains[:, m, :], in_=g_ps[:])
+
         vec = sb([P, 52], F32, "vec")
-        nc.scalar.copy(out=vec[:], in_=sm_ps[:, 0:52])
+
+        def small_vectors():
+            sm_ps = tr_bank("sm_ps", BF16)
+            nc.tensor.transpose(sm_ps[:, 0:P], small[:], ident_bf[:])
+            nc.scalar.copy(out=vec[:], in_=sm_ps[:, 0:52])
 
         grouped = [sb([P, 4096], BF16, "grouped%d" % m) for m in range(3)]
         u_codes = [sb([P, 1024], U32, "u_codes%d" % m) for m in range(3)]
@@ -140,7 +143,8 @@ def tile_visionpermutatorsegmentmixing_kernel(tc, x, g, w, b, ka, gp, wp_bytes, 
         t_banks = {}
         full = slice(0, 512)
 
-        def gain(m, q):
+        def gain(m, q, part=None):
+            z = slice(0, 16) if part is None else slice(8 * part, 8 * part + 8)
             if m == 2:
                 nc.vector.tensor_tensor(
                     out=u[2][:, 2 * q : 2 * q + 2, :],
@@ -149,10 +153,12 @@ def tile_visionpermutatorsegmentmixing_kernel(tc, x, g, w, b, ka, gp, wp_bytes, 
                     op=MULT,
                 )
             else:
+                size = z.stop - z.start
+                gain_z = gains[:, m, :].rearrange("p (z e) -> p z e", e=32)[:, z, :]
                 nc.vector.tensor_tensor(
-                    out=u[m][:, q:8:4, :].rearrange("p s (z e) -> p s z e", e=32),
-                    in0=xs[m][:].rearrange("p z (s e) -> p s z e", e=32)[:, q:8:4, :, :],
-                    in1=gains[:, m, :].rearrange("p (z e) -> p z e", e=32).unsqueeze(1).to_broadcast([P, 2, 16, 32]),
+                    out=u[m][:, 2 * q : 2 * q + 2, :].rearrange("p s (z e) -> p s z e", e=32)[:, :, z, :],
+                    in0=xs[m][:].rearrange("p z (s e) -> p s z e", e=32)[:, q:8:4, z, :],
+                    in1=gain_z.unsqueeze(1).to_broadcast([P, 2, size, 32]),
                     op=MULT,
                 )
 
@@ -163,22 +169,23 @@ def tile_visionpermutatorsegmentmixing_kernel(tc, x, g, w, b, ka, gp, wp_bytes, 
             words = u[m][:].bitcast(F32)
             for t in range(2):
                 for v in range(2):
-                    row = 2 * q + t if m == 2 else q + 4 * t
-                    nc.tensor.transpose(view[:, v, t, :], words[:, row, v::2], perms[m][:])
+                    nc.tensor.transpose(view[:, v, t, :], words[:, 2 * q + t, v::2], perms[m][:])
 
         def evac(m, q):
             ps = t_banks[m, q]
             words = grouped[m][:].bitcast(F32)
-            if m == 1:
-                nc.scalar.copy(
-                    out=words[:, 512 * q : 512 * q + 512].rearrange("p (c u) -> p c u", u=2),
-                    in_=ps[:].rearrange("p (u c) -> p c u", u=2),
-                )
-            elif m == 0:
-                nc.scalar.copy(
-                    out=words.rearrange("p (k q r u) -> p k q r u", q=4, r=32, u=2)[:, :, q, :, :],
-                    in_=ps[:].rearrange("p (u k r) -> p k r u", u=2, r=32),
-                )
+            if m < 2:
+                src = ps[:].rearrange("p (u f h n c) -> p n (f h) c u", u=2, f=2, h=2, n=2)
+                for n in range(2):
+                    if m == 1:
+                        dst = words[:, 512 * q + 256 * n : 512 * q + 256 * n + 256]
+                    elif n == 0:
+                        dst = words[:, 256 * q : 256 * q + 256]
+                    if m == 0 and n == 1:
+                        dst = words[:, 1024:].rearrange("p (k q c u) -> p q k c u", k=4, q=4, u=2)[:, q, :, :, :]
+                    else:
+                        dst = dst.rearrange("p (k c u) -> p k c u", k=4, u=2)
+                    nc.scalar.copy(out=dst, in_=src[:, n, :, :, :])
             else:
                 nc.scalar.copy(
                     out=words.rearrange("p (n x l y u) -> p n l x y u", n=2, x=4, l=2, u=2)[:, q // 2, q % 2, :, :, :],
@@ -226,10 +233,10 @@ def tile_visionpermutatorsegmentmixing_kernel(tc, x, g, w, b, ka, gp, wp_bytes, 
             lc, ls, rc, rs = (w_c, w_s, u_c, u_s) if w_stationary else (u_c, u_s, w_c, w_s)
             mx_raw(o, lc[:, lcols], ls[:, lcols], rc[:, rcols], rs[:, rcols], start, stop)
 
-        red = [sb([P, 8, 4, 2], F32, "red%d" % m) for m in range(2)]
+        red = [sb([P, 4, 16], F32, "red%d" % m) for m in range(2)]
 
         def pool_mm(m, half):
-            ps = pa_bank("pa%d_%d" % (m, half))
+            ps = bank("pa%d_%d" % (m, half))
             t_banks["pool", m, half] = ps
             for z in range(4):
                 mx(ps[:], m, slice(128 * z, 128 * z + 128), slice(512 * half, 512 * half + 512), True, z == 0, z == 3)
@@ -237,10 +244,13 @@ def tile_visionpermutatorsegmentmixing_kernel(tc, x, g, w, b, ka, gp, wp_bytes, 
         def pool_red(m, half):
             ps = t_banks["pool", m, half]
             if m == 1:
-                dst = red[1][:].rearrange("p k q l -> p q k l")[:, 2 * half : 2 * half + 2, :, :]
-                src = ps[:].rearrange("p (q k l y) -> p q k l y", q=2, k=8, l=2)
+                dst = red[1][:, 2 * half : 2 * half + 2, :]
+                src = ps[:].rearrange("p (q k y) -> p q k y", q=2, y=16)
+            elif half == 0:
+                dst = red[0][:, :, 0:8]
+                src = ps[:].rearrange("p (q k y) -> p q k y", q=4, y=16)
             else:
-                dst = red[0][:, 4 * half : 4 * half + 4, :, :]
+                dst = red[0][:].rearrange("p q (n k l) -> p n k q l", n=2, l=2)[:, 1, :, :, :]
                 src = ps[:].rearrange("p (k q l y) -> p k q l y", k=4, q=4, l=2)
             nc.vector.tensor_reduce(out=dst, in_=src, axis=AX, op=ADD)
 
@@ -256,61 +266,102 @@ def tile_visionpermutatorsegmentmixing_kernel(tc, x, g, w, b, ka, gp, wp_bytes, 
         def pool2_out(n):
             nc.scalar.copy(out=pb_sb[:, n, :], in_=t_banks["pb", n][:])
 
-        def pad_moves():
+        def pad_moves(m):
             nc.vector.tensor_copy(
-                out=pad_codes[:, :, 96:128].bitcast(I32),
-                in_=w_codes[1][:].rearrange("p (z e) -> p z e", e=32).bitcast(I32),
+                out=pad_codes[m][:, 96:].rearrange("p (z c) -> p z c", c=128)[:, :, 0:32].bitcast(I32),
+                in_=w_codes[m][:].rearrange("p (z e) -> p z e", e=32).bitcast(I32),
             )
-            for q in range(4):
-                nc.vector.tensor_copy(
-                    out=pad_scales[:].rearrange("p q z x -> p (q z x)").bitcast(I32).rearrange(
-                        "p (q z x) -> p q z x", q=4, z=16
-                    )[:, q, :, 8 * q : 8 * q + 8],
-                    in_=w_scales[1][:].bitcast(I32).rearrange("p (z x) -> p z x", x=8),
-                )
+            nc.vector.tensor_copy(
+                out=pad_scales[m][1][:, 160:672].bitcast(I32), in_=pad_scales[m][0][:, 128:640].bitcast(I32)
+            )
 
-        y0 = sb([P, 8, 16, 32], F32, "y0")
-        y1 = sb([P, 16, 16, 16], F32, "y1")
+        y01 = [[sb([P, 16, 8, 16], F32, "y%d_%d" % (m, n)) for n in range(1 + m)] for m in range(2)]
+        y0s = sb([P, 4, 16, 32], F32, "y0s")
 
-        def y1_mm(pair):
-            ps = ym_bank("ym%d" % pair)
-            t_banks["y1", pair] = ps
-            for d in range(2):
-                z = 2 * pair + d
+        def swap_mm(k):
+            ps = bank("ys%d" % k)
+            t_banks["ys", k] = ps
+            mx(ps[:], 0, slice(512 + 128 * k, 640 + 128 * k), full, False)
+
+        def swap_out(k):
+            nc.vector.transpose(out=y0s[:, k, :, :].rearrange("p z r -> p (z r)"), in_=t_banks["ys", k][:])
+
+        def swap_bias(k):
+            nc.vector.tensor_tensor(
+                out=y0s[:, k, :, :],
+                in0=y0s[:, k, :, :],
+                in1=vec[:, 0:16].unsqueeze(2).to_broadcast([P, 16, 32]),
+                op=ADD,
+            )
+
+        def y_mm(m, nh, quad):
+            ps = bank("ym%d_%d_%d" % (m, nh, quad))
+            t_banks["y", m, nh, quad] = ps
+            for d in range(4):
+                z = 4 * quad + d
                 for q in range(4):
+                    c0 = 256 * q + 128 * nh if m == 1 else 128 * q
+                    cols = slice(c0, c0 + 128)
+                    start = 96 + 128 * z - 32 * q
+                    odd = (z - q) % 2
+                    s_start = 128 + 32 * (z - q + odd)
                     mx_raw(
-                        ps[:, 256 * d : 256 * d + 256],
-                        pad_codes[:, z, 96 - 32 * q : 224 - 32 * q],
-                        pad_scales[:, q, z, :],
-                        u_codes[1][:, 256 * q : 256 * q + 256],
-                        u_scales[1][:, 256 * q : 256 * q + 256],
+                        ps[:, 128 * d : 128 * d + 128],
+                        pad_codes[m][:, start : start + 128],
+                        pad_scales[m][odd][:, s_start : s_start + 128],
+                        u_codes[m][:, cols],
+                        u_scales[m][:, cols],
                         q == 0,
                         q == 3,
                     )
 
-        def y1_out(pair):
-            ps = t_banks["y1", pair]
-            for d in range(2):
-                z = 2 * pair + d
+        def y_out(m, nh, quad, eng="s"):
+            ps = t_banks["y", m, nh, quad]
+            for d in range(4):
+                z = 4 * quad + d
+                if eng == "v":
+                    nc.vector.tensor_scalar(
+                        out=y01[m][nh][:, z, :, :].rearrange("p k y -> p (k y)"),
+                        in0=ps[:, 128 * d : 128 * d + 128],
+                        scalar1=vec[:, 16 * m + z : 16 * m + z + 1],
+                        scalar2=None,
+                        op0=ADD,
+                    )
+                    continue
                 nc.scalar.activation(
-                    out=y1[:, z, :, :].rearrange("p k i -> p (k i)"),
-                    in_=ps[:, 256 * d : 256 * d + 256],
+                    out=y01[m][nh][:, z, :, :].rearrange("p k y -> p (k y)"),
+                    in_=ps[:, 128 * d : 128 * d + 128],
                     func=ACT.Identity,
-                    bias=vec[:, 16 + z : 17 + z],
+                    bias=vec[:, 16 * m + z : 16 * m + z + 1],
                 )
 
-        def y0_mm(k):
-            ps = mm_bank("y0_%d" % k)
-            t_banks["y0", k] = ps
-            mx(ps[:], 0, slice(128 * k, 128 * k + 128), full, False)
-
-        def y0_out(k):
-            nc.vector.transpose(out=y0[:, k, :, :].rearrange("p z r -> p (z r)"), in_=t_banks["y0", k][:])
-
-        def y0_bias(z):
-            nc.vector.tensor_scalar(
-                out=y0[:, :, z, :], in0=y0[:, :, z, :], scalar1=vec[:, z : z + 1], scalar2=None, op0=ADD
-            )
+        def y_both(m, pair):
+            ps = bank("yb%d_%d" % (m, pair))
+            for d in range(2):
+                z = 2 * pair + d
+                for q in range(4):
+                    cols = slice(256 * q, 256 * q + 256)
+                    start = 96 + 128 * z - 32 * q
+                    odd = (z - q) % 2
+                    s_start = 128 + 32 * (z - q + odd)
+                    mx_raw(
+                        ps[:, 256 * d : 256 * d + 256],
+                        pad_codes[m][:, start : start + 128],
+                        pad_scales[m][odd][:, s_start : s_start + 128],
+                        u_codes[m][:, cols],
+                        u_scales[m][:, cols],
+                        q == 0,
+                        q == 3,
+                    )
+            for n in range(2):
+                for d in range(2):
+                    z = 2 * pair + d
+                    nc.scalar.activation(
+                        out=y01[m][n][:, z, :, :].rearrange("p k y -> p (k y)"),
+                        in_=ps[:, 256 * d + 128 * n : 256 * d + 128 * n + 128],
+                        func=ACT.Identity,
+                        bias=vec[:, 16 * m + z : 16 * m + z + 1],
+                    )
 
         b_mean = sb([P, 1], F32, "b_mean")
         b_pool = sb([P, 4], F32, "b_pool")
@@ -337,31 +388,10 @@ def tile_visionpermutatorsegmentmixing_kernel(tc, x, g, w, b, ka, gp, wp_bytes, 
         amp = sb([P, 3, 16], F32, "amp")
         a2b2 = sb([P, 4, 4], F32, "a2b2")
 
-        def softmax():
-            sel_ps = tr_bank("sel_ps")
-            for m in range(2):
-                nc.tensor.matmul(
-                    sel_ps[:, 0:64],
-                    lhsT=e_sel[:],
-                    rhs=red[m][:].rearrange("p k q l -> p (k q l)"),
-                    start=(m == 0),
-                    stop=(m == 1),
-                )
-            picked = sb([P, 8, 4, 2], F32, "picked")
-            nc.vector.tensor_tensor(
-                out=picked[:],
-                in0=sel_ps[:, 0:64].rearrange("p (k q l) -> p k q l", k=8, q=4),
-                in1=q_mask[:].unsqueeze(1).unsqueeze(3).to_broadcast([P, 8, 4, 2]),
-                op=MULT,
-            )
-            pool01 = sb([P, 2, 2, 2, 2], F32, "pool01")
-            nc.vector.tensor_reduce(
-                out=pool01[:].rearrange("p f h n l -> p (f h n) l"),
-                in_=picked[:].rearrange("p k q l -> p k l q"),
-                axis=AX,
-                op=ADD,
-            )
-            p2_ps = tr_bank("p2_ps")
+        chain = {}
+
+        def pool2_sum():
+            p2_ps = bank("p2_ps")
             for c in range(4):
                 for n in range(2):
                     k = 4 * c + 2 * n
@@ -379,51 +409,89 @@ def tile_visionpermutatorsegmentmixing_kernel(tc, x, g, w, b, ka, gp, wp_bytes, 
                 in1=b_pool[:].unsqueeze(2).to_broadcast([P, 4, 4]),
                 op=ADD,
             )
-            pool = sb([P, 4, 4], F32, "pool")
-            nc.vector.tensor_tensor(
-                out=pool[:].rearrange("p (h f) n -> p h f n", h=2),
-                in0=pool_a[:].rearrange("p (h f) n -> p h f n", h=2),
-                in1=pool01[:].rearrange("p f h n l -> p h f (n l)"),
-                op=ADD,
-            )
-            logit = sb([P, 3, 16], F32, "logit")
-            nc.vector.tensor_tensor(
-                out=logit[:].rearrange("p m (c n) -> p m c n", c=4),
-                in0=pool[:].unsqueeze(1).to_broadcast([P, 3, 4, 4]),
-                in1=vec[:, 36:48].rearrange("p (m c) -> p m c", m=3).unsqueeze(3).to_broadcast([P, 3, 4, 4]),
-                op=MULT,
-            )
-            l_max = sb([P, 16], F32, "l_max")
-            nc.vector.tensor_reduce(out=l_max[:], in_=logit[:].rearrange("p m k -> p k m"), axis=AX, op=MAX)
-            shifted = sb([P, 3, 16], F32, "shifted")
-            nc.vector.tensor_tensor(
-                out=shifted[:], in0=logit[:], in1=l_max[:].unsqueeze(1).to_broadcast([P, 3, 16]), op=SUB
-            )
-            expo = sb([P, 3, 16], F32, "expo")
-            nc.scalar.activation(out=expo[:], in_=shifted[:], func=ACT.Exp)
-            e_tot = sb([P, 16], F32, "e_tot")
-            nc.vector.tensor_reduce(out=e_tot[:], in_=expo[:].rearrange("p m k -> p k m"), axis=AX, op=ADD)
-            e_inv = sb([P, 16], F32, "e_inv")
-            nc.vector.reciprocal(out=e_inv[:], in_=e_tot[:])
-            e_gp = sb([P, 4, 4], F32, "e_gp")
-            nc.vector.tensor_tensor(
-                out=e_gp[:],
-                in0=e_inv[:].rearrange("p (c n) -> p c n", c=4),
-                in1=vec[:, 48:52].unsqueeze(2).to_broadcast([P, 4, 4]),
-                op=MULT,
-            )
-            nc.vector.tensor_tensor(
-                out=amp[:],
-                in0=expo[:],
-                in1=e_gp[:].rearrange("p c n -> p (c n)").unsqueeze(1).to_broadcast([P, 3, 16]),
-                op=MULT,
-            )
-            nc.vector.tensor_tensor(
-                out=a2b2[:],
-                in0=amp[:, 2, :].rearrange("p (c n) -> p c n", c=4),
-                in1=vec[:, 32:36].unsqueeze(2).to_broadcast([P, 4, 4]),
-                op=MULT,
-            )
+            chain["pool_a"] = pool_a
+
+        def pool01_sum():
+            sel_ps = bank("sel_ps")
+            for m in range(2):
+                for q in range(4):
+                    nc.tensor.matmul(
+                        sel_ps[:, 0:16],
+                        lhsT=e_sel[:, q, :],
+                        rhs=red[m][:, q, :],
+                        start=(m == 0 and q == 0),
+                        stop=(m == 1 and q == 3),
+                    )
+            chain["sel"] = sel_ps
+
+        def softmax(step):
+            if step == 0:
+                pool = sb([P, 4, 4], F32, "pool")
+                for n in range(2):
+                    nc.vector.tensor_tensor(
+                        out=pool[:].rearrange("p (h f) (n l) -> p n f h l", h=2, n=2)[:, n, :, :, :],
+                        in0=chain["sel"][:, 0:16].rearrange("p (n f h l) -> p n f h l", n=2, f=2, h=2)[:, n, :, :, :],
+                        in1=chain["pool_a"][:].rearrange("p (h f) (n l) -> p n f h l", h=2, n=2)[:, n, :, :, :],
+                        op=ADD,
+                    )
+                chain["pool"] = pool
+            elif step == 1:
+                logit = sb([P, 3, 16], F32, "logit")
+                nc.vector.tensor_tensor(
+                    out=logit[:].rearrange("p m (c n) -> p m c n", c=4),
+                    in0=chain["pool"][:].unsqueeze(1).to_broadcast([P, 3, 4, 4]),
+                    in1=vec[:, 36:48].rearrange("p (m c) -> p m c", m=3).unsqueeze(3).to_broadcast([P, 3, 4, 4]),
+                    op=MULT,
+                )
+                chain["logit"] = logit
+            elif step == 2:
+                l_max = sb([P, 16], F32, "l_max")
+                nc.vector.tensor_reduce(
+                    out=l_max[:], in_=chain["logit"][:].rearrange("p m k -> p k m"), axis=AX, op=MAX
+                )
+                chain["max"] = l_max
+            elif step == 3:
+                shifted = sb([P, 3, 16], F32, "shifted")
+                nc.vector.tensor_tensor(
+                    out=shifted[:],
+                    in0=chain["logit"][:],
+                    in1=chain["max"][:].unsqueeze(1).to_broadcast([P, 3, 16]),
+                    op=SUB,
+                )
+                expo = sb([P, 3, 16], F32, "expo")
+                nc.scalar.activation(out=expo[:], in_=shifted[:], func=ACT.Exp)
+                chain["expo"] = expo
+            elif step == 4:
+                e_tot = sb([P, 16], F32, "e_tot")
+                nc.vector.tensor_reduce(
+                    out=e_tot[:], in_=chain["expo"][:].rearrange("p m k -> p k m"), axis=AX, op=ADD
+                )
+                e_gp = sb([P, 3, 4, 4], F32, "e_gp")
+                nc.vector.tensor_tensor(
+                    out=e_gp[:],
+                    in0=chain["expo"][:].rearrange("p m (c n) -> p m c n", c=4),
+                    in1=vec[:, 48:52].unsqueeze(1).unsqueeze(3).to_broadcast([P, 3, 4, 4]),
+                    op=MULT,
+                )
+                chain["tot"], chain["gp"] = e_tot, e_gp
+            elif step == 5:
+                e_inv = sb([P, 16], F32, "e_inv")
+                nc.vector.reciprocal(out=e_inv[:], in_=chain["tot"][:])
+                chain["inv"] = e_inv
+            elif step == 6:
+                nc.vector.tensor_tensor(
+                    out=amp[:],
+                    in0=chain["gp"][:].rearrange("p m c n -> p m (c n)"),
+                    in1=chain["inv"][:].unsqueeze(1).to_broadcast([P, 3, 16]),
+                    op=MULT,
+                )
+            else:
+                nc.vector.tensor_tensor(
+                    out=a2b2[:],
+                    in0=amp[:, 2, :].rearrange("p (c n) -> p c n", c=4),
+                    in1=vec[:, 32:36].unsqueeze(2).to_broadcast([P, 4, 4]),
+                    op=MULT,
+                )
 
         f_sb = keep.tile([P, 4, 4, 256], BF16, name="f_sb", tag="u0", align_bytes=64)
 
@@ -448,30 +516,30 @@ def tile_visionpermutatorsegmentmixing_kernel(tc, x, g, w, b, ka, gp, wp_bytes, 
                     bias=a2b2[:, c, 2 * nh + l : 2 * nh + l + 1],
                 )
 
-        def combine23(n, pair):
+        def combine23(n, chunks, h=None):
             nh, l = n // 2, n % 2
-            v2 = []
-            for c in (2 * pair, 2 * pair + 1):
-                f, h = c % 2, c // 2
+            rows = slice(0, 16) if h is None else slice(8 * h, 8 * h + 8)
+            for c in chunks:
                 k = 4 * c + n
-                t = work.tile([P, 16, 16], F32, name="v2")
-                v2.append(t)
+                if nh == 0:
+                    in0 = y01[0][0][:, rows, 4 * (c % 2) + 2 * (c // 2) + l, :]
+                else:
+                    in0 = y0s[:, 2 * (c % 2) + c // 2, rows, 16 * l : 16 * l + 16]
                 nc.vector.scalar_tensor_tensor(
-                    out=t[:],
-                    in0=y0[:, 4 * f + 2 * h + nh, :, 16 * l : 16 * l + 16],
+                    out=v1_tiles[c, n][:, rows, :],
+                    in0=in0,
                     scalar=amp[:, 0, k : k + 1],
-                    in1=v1_tiles[c, n][:],
+                    in1=v1_tiles[c, n][:, rows, :],
                     op0=MULT,
                     op1=ADD,
                 )
-            for c in (2 * pair, 2 * pair + 1):
-                f, h = c % 2, c // 2
+            for c in chunks:
                 k = 4 * c + n
                 nc.vector.scalar_tensor_tensor(
-                    out=f_sb[:, c, n, :].rearrange("p (i j) -> p i j", i=16),
-                    in0=y1[:, :, 8 * f + 4 * h + n, :].rearrange("p j i -> p i j"),
+                    out=f_sb[:, c, n, :].rearrange("p (i j) -> p i j", i=16)[:, rows, :],
+                    in0=y01[1][nh][:, :, 4 * (c % 2) + 2 * (c // 2) + l, rows].rearrange("p j i -> p i j"),
                     scalar=amp[:, 1, k : k + 1],
-                    in1=v2[c % 2][:],
+                    in1=v1_tiles[c, n][:, rows, :],
                     op0=MULT,
                     op1=ADD,
                 )
@@ -499,114 +567,185 @@ def tile_visionpermutatorsegmentmixing_kernel(tc, x, g, w, b, ka, gp, wp_bytes, 
             )
             f_tiles[n, h] = fg
 
-        def f_project(n, h):
+        def f_project(n, h, eng="s"):
             f_codes = work.tile([P, 128], U32, name="f_codes", align_bytes=64)
             f_scales = work.tile([P, 128], U8, name="f_scales", align_bytes=64)
             nc.vector.quantize_mx(out=f_codes[:].bitcast(FP8X4), scales=f_scales[:], in_=f_tiles[n, h][:])
             po = pa_bank("po%d_%d" % (n, h))
             mx_raw(po[:], f_codes[:], f_scales[:], w_codes[3][:], w_scales[3][:], True, True)
             res = work.tile([P, 512], F32, name="res", bufs=4)
-            nc.scalar.copy(out=res[:], in_=po[:])
+            if eng == "s":
+                nc.scalar.copy(out=res[:], in_=po[:])
+            else:
+                nc.vector.tensor_copy(out=res[:], in_=po[:])
             nc.sync.dma_start(out=out[n].rearrange("i j c -> (i j) c")[128 * h : 128 * h + 128, :], in_=res[:])
 
         with tc.manual_schedule():
-            for q in range(2):
-                gain(2, q)
-                turn(2, q)
-                evac(2, q)
-            for q in range(4):
-                gain(1, q)
-                turn(1, q)
-                evac(1, q)
+            gain(1, 0, 0)
+            gain(1, 1, 0)
+            gain(1, 3, 0)
+            gain(1, 2, 0)
+            gain(1, 1, 1)
+            turn(1, 1)
+            gain(1, 3, 1)
+            gain(1, 2, 1)
+            turn(1, 3)
+            evac(1, 3)
             w_inter(1, "v", 1)
-            w_inter(1, "s", 0)
-            for q in range(2, 4):
-                gain(2, q)
-                turn(2, q)
-                evac(2, q)
-            quant_u(1, 0)
-            quant_u(1, 1)
+            gain(1, 0, 1)
+            gain(2, 1)
+            turn(1, 0)
+            turn(1, 2)
+            gain(2, 0)
+            w_inter(1, "v", 0)
+            turn(2, 1)
+            evac(1, 2)
+            turn(2, 0)
+            gain(2, 2)
+            gain(2, 3)
             w_quant(1)
-            pad_moves()
-            pool_mm(1, 0)
-            gain(0, 0)
-            turn(0, 0)
-            evac(0, 0)
-            gain(0, 1)
-            turn(0, 1)
-            evac(0, 1)
-            pool_mm(1, 1)
+            turn(2, 3)
+            evac(1, 1)
             gain(0, 2)
-            turn(0, 2)
-            evac(0, 2)
+            evac(1, 0)
+            evac(2, 1)
+            gain(0, 0)
+            evac(2, 0)
+            small_vectors()
+            evac(2, 3)
             gain(0, 3)
+            gain(0, 1)
+            quant_u(1, 1)
+            turn(2, 2)
+            quant_u(1, 0)
+            w_inter(2, "s", 0)
+            w_inter(2, "s", 1)
+            turn(0, 2)
+            turn(0, 0)
             turn(0, 3)
-            evac(0, 3)
-            w_inter(0, "s", 0)
-            w_inter(2, "g", 0)
-            w_inter(2, "g", 1)
+            turn(0, 1)
             quant_u(2, 0)
+            evac(2, 2)
+            pool_mm(1, 1)
+            evac(0, 2)
+            pool_mm(1, 0)
+            pad_moves(1)
+            evac(0, 3)
             quant_u(2, 1)
-            pool_red(1, 0)
+            w_inter(0, "s", 0)
+            w_quant(2)
             pool_red(1, 1)
             w_inter(0, "v", 1)
-            for k in range(3):
-                y1_mm(k)
-                y1_out(k)
-            quant_u(0, 0)
-            quant_u(0, 1)
-            w_quant(2)
+            evac(0, 0)
+            evac(0, 1)
+            y_both(1, 3)
+            wp_widen(1)
+            y_both(1, 1)
             w_quant(0)
+            y_both(1, 0)
+            quant_u(0, 0)
             pool2_mm(0)
-            pool2_out(0)
-            y0_mm(0)
-            y0_mm(1)
-            pool2_mm(1)
-            pool2_out(1)
-            for j in range(4):
-                wp_widen(j)
-            w_inter(3, "g", 0)
-            w_inter(3, "g", 1)
-            bias_mean()
-            y0_out(0)
-            y0_out(1)
-            for k in range(2, 4):
-                y0_mm(k)
-                y0_out(k)
+            quant_u(0, 1)
             pool_mm(0, 0)
-            for k in range(4, 6):
-                y0_mm(k)
-                y0_out(k)
             pool_mm(0, 1)
-            pool_red(0, 0)
-            for k in range(6, 8):
-                y0_mm(k)
-                y0_out(k)
+            wp_widen(3)
+            pool_red(1, 0)
+            pad_moves(0)
+            pool2_out(0)
             pool_red(0, 1)
-            y1_mm(3)
-            y1_out(3)
-            softmax()
-            for z in range(16):
-                y0_bias(z)
-            for k in range(4, 8):
-                y1_mm(k)
-                y1_out(k)
-                y2_mm(0, k - 4)
-                combine1(0, k - 4)
-            for c in range(4):
-                y2_mm(1, c)
-                combine1(1, c)
-            for n in range(4):
-                for pair in range(2):
-                    combine23(n, pair)
-                    if n >= 2:
-                        f_project(n - 2, pair)
-                if n == 1:
-                    w_quant(3)
-                for h in range(2):
-                    f_turn_a(n, h)
-                for h in range(2):
-                    f_turn_b(n, h)
-            for n in range(2, 4):
-                for h in range(2):
-                    f_project(n, h)
+            pool2_mm(1)
+            wp_widen(0)
+            pool_red(0, 0)
+            swap_mm(3)
+            swap_mm(2)
+            bias_mean()
+            swap_out(2)
+            y_mm(0, 0, 1)
+            pool2_out(1)
+            swap_mm(1)
+            pool01_sum()
+            swap_out(3)
+            pool2_sum()
+            wp_widen(2)
+            softmax(0)
+            y_mm(0, 0, 3)
+            w_inter(3, "s", 1)
+            swap_out(1)
+            softmax(1)
+            swap_mm(0)
+            y_out(0, 0, 3)
+            softmax(2)
+            y_out(0, 0, 1)
+            softmax(3)
+            y_mm(0, 0, 0)
+            y2_mm(0, 0)
+            softmax(4)
+            y_mm(0, 0, 2)
+            w_inter(3, "s", 0)
+            y_mm(1, 0, 3)
+            swap_bias(1)
+            y2_mm(0, 1)
+            softmax(5)
+            y_mm(1, 0, 2)
+            softmax(6)
+            y_out(0, 0, 0)
+            softmax(7)
+            combine1(0, 0)
+            y_out(0, 0, 2)
+            combine1(0, 1)
+            y_out(1, 0, 2)
+            swap_bias(2)
+            w_quant(3)
+            swap_out(0)
+            y_out(1, 0, 3)
+            y_both(1, 2)
+            swap_bias(0)
+            y2_mm(0, 2)
+            swap_bias(3)
+            y2_mm(0, 3)
+            y2_mm(1, 3)
+            y2_mm(1, 2)
+            y_mm(1, 1, 3)
+            combine1(0, 2)
+            combine23(1, (0, 1))
+            y2_mm(1, 0)
+            combine23(0, (0, 1))
+            combine1(0, 3)
+            combine23(0, (2, 3))
+            combine1(1, 3)
+            combine1(1, 2)
+            y_mm(1, 1, 2)
+            y2_mm(1, 1)
+            y_out(1, 1, 3)
+            combine23(1, (2, 3))
+            combine1(1, 0)
+            y_out(1, 1, 2)
+            f_turn_a(0, 1)
+            f_turn_a(0, 0)
+            combine1(1, 1)
+            f_turn_a(1, 1)
+            combine23(2, (2, 3))
+            combine23(3, (0, 1, 2, 3), 1)
+            f_turn_a(1, 0)
+            f_turn_b(0, 1)
+            f_turn_b(0, 0)
+            f_turn_b(1, 0)
+            f_turn_b(1, 1)
+            f_turn_a(3, 1)
+            f_project(0, 1)
+            f_project(0, 0)
+            combine23(3, (0, 1, 2, 3), 0)
+            f_turn_b(3, 1)
+            f_turn_a(3, 0)
+            f_project(1, 1)
+            f_project(1, 0)
+            f_turn_b(3, 0)
+            combine23(2, (0, 1))
+            f_turn_a(2, 1)
+            f_turn_a(2, 0)
+            f_project(3, 1, "v")
+            f_turn_b(2, 1)
+            f_turn_b(2, 0)
+            f_project(3, 0, "s")
+            f_project(2, 1)
+            f_project(2, 0)

@@ -98,6 +98,11 @@ def tile_visionpermutatorsegmentmixing_kernel(tc, x, g, w, b, ka, gp, wp_bytes, 
             out=perm0[:].rearrange("p (h n y) -> p h n y", h=2, n=4),
             in_=ident[:].rearrange("p (y h n) -> p h n y", h=2, n=4),
         )
+        perm_f = sb([P, P], F32, "perm_f")
+        nc.vector.tensor_copy(
+            out=perm_f[:].rearrange("p (b a j) -> p b a j", a=2, b=4),
+            in_=ident[:].rearrange("p (a b j) -> p b a j", a=2, b=4),
+        )
         perm1 = sb([P, P], F32, "perm1")
         nc.vector.tensor_copy(
             out=perm1[:].rearrange("p (h y) -> p h y", h=2),
@@ -117,7 +122,8 @@ def tile_visionpermutatorsegmentmixing_kernel(tc, x, g, w, b, ka, gp, wp_bytes, 
         for m in (1, 0):
             for k in range(2):
                 nc.vector.memset(pad_scales[m][k][:].bitcast(I32), 0)
-            nc.gpsimd.memset(pad_codes[m][:].bitcast(I32), 0)
+            pad_engine = nc.vector if m == 1 else nc.gpsimd
+            pad_engine.memset(pad_codes[m][:].bitcast(I32), 0)
         warm = sb([P, 1], F32, "warm")
         nc.scalar.activation(out=warm[:], in_=e_sum[:, 0:1], func=ACT.Exp)
 
@@ -207,7 +213,11 @@ def tile_visionpermutatorsegmentmixing_kernel(tc, x, g, w, b, ka, gp, wp_bytes, 
             n = 512 // parts
             src = (w_raw + [wp_w])[m]
             dst = w_groups[m][:, n * h : n * h + n, :]
-            src = src[:, :, n * h : n * h + n].rearrange("p j n -> p n j")
+            if m == 0:
+                dst = dst.rearrange("p (a b e) j -> p a b e j", a=2, b=4)
+                src = src.rearrange("p j (b a e) -> p a b e j", a=4, b=4)[:, 2 * h : 2 * h + 2, :, :, :]
+            else:
+                src = src[:, :, n * h : n * h + n].rearrange("p j n -> p n j")
             if eng == "s":
                 nc.scalar.copy(out=dst, in_=src)
             elif eng == "v":
@@ -275,7 +285,17 @@ def tile_visionpermutatorsegmentmixing_kernel(tc, x, g, w, b, ka, gp, wp_bytes, 
                 out=pad_scales[m][1][:, 160:672].bitcast(I32), in_=pad_scales[m][0][:, 128:640].bitcast(I32)
             )
 
-        y01 = [[sb([P, 16, 8, 16], F32, "y%d_%d" % (m, n)) for n in range(1 + m)] for m in range(2)]
+        y0m = sb([P, 16, 8, 16], F32, "y0m")
+        y1 = [sb([P, 4, 16, 8, 4], F32, "y1_%d" % n) for n in range(2)]
+
+        def y_dst(m, nh, z):
+            if m == 0:
+                return y0m[:, z, :, :].rearrange("p k (b a) -> p k b a", b=4)
+            return y1[nh][:, :, z, :, :].rearrange("p b k a -> p k b a")
+
+        def y_bias(m, z):
+            i = 4 * (z % 4) + z // 4 if m == 0 else 16 + z
+            return vec[:, i : i + 1]
         y0s = sb([P, 4, 16, 32], F32, "y0s")
 
         def swap_mm(k):
@@ -288,9 +308,9 @@ def tile_visionpermutatorsegmentmixing_kernel(tc, x, g, w, b, ka, gp, wp_bytes, 
 
         def swap_bias(k):
             nc.vector.tensor_tensor(
-                out=y0s[:, k, :, :],
-                in0=y0s[:, k, :, :],
-                in1=vec[:, 0:16].unsqueeze(2).to_broadcast([P, 16, 32]),
+                out=y0s[:, k, :, :].rearrange("p (a b) r -> p a b r", a=4),
+                in0=y0s[:, k, :, :].rearrange("p (a b) r -> p a b r", a=4),
+                in1=vec[:, 0:16].rearrange("p (b a) -> p a b", b=4).unsqueeze(3).to_broadcast([P, 4, 4, 32]),
                 op=ADD,
             )
 
@@ -315,24 +335,15 @@ def tile_visionpermutatorsegmentmixing_kernel(tc, x, g, w, b, ka, gp, wp_bytes, 
                         q == 3,
                     )
 
-        def y_out(m, nh, quad, eng="s"):
+        def y_out(m, nh, quad):
             ps = t_banks["y", m, nh, quad]
             for d in range(4):
                 z = 4 * quad + d
-                if eng == "v":
-                    nc.vector.tensor_scalar(
-                        out=y01[m][nh][:, z, :, :].rearrange("p k y -> p (k y)"),
-                        in0=ps[:, 128 * d : 128 * d + 128],
-                        scalar1=vec[:, 16 * m + z : 16 * m + z + 1],
-                        scalar2=None,
-                        op0=ADD,
-                    )
-                    continue
                 nc.scalar.activation(
-                    out=y01[m][nh][:, z, :, :].rearrange("p k y -> p (k y)"),
-                    in_=ps[:, 128 * d : 128 * d + 128],
+                    out=y_dst(m, nh, z),
+                    in_=ps[:, 128 * d : 128 * d + 128].rearrange("p (k b a) -> p k b a", k=8, b=4),
                     func=ACT.Identity,
-                    bias=vec[:, 16 * m + z : 16 * m + z + 1],
+                    bias=y_bias(m, z),
                 )
 
         def y_both(m, pair):
@@ -357,10 +368,12 @@ def tile_visionpermutatorsegmentmixing_kernel(tc, x, g, w, b, ka, gp, wp_bytes, 
                 for d in range(2):
                     z = 2 * pair + d
                     nc.scalar.activation(
-                        out=y01[m][n][:, z, :, :].rearrange("p k y -> p (k y)"),
-                        in_=ps[:, 256 * d + 128 * n : 256 * d + 128 * n + 128],
+                        out=y_dst(m, n, z),
+                        in_=ps[:, 256 * d + 128 * n : 256 * d + 128 * n + 128].rearrange(
+                            "p (k b a) -> p k b a", k=8, b=4
+                        ),
                         func=ACT.Identity,
-                        bias=vec[:, 16 * m + z : 16 * m + z + 1],
+                        bias=y_bias(m, z),
                     )
 
         b_mean = sb([P, 1], F32, "b_mean")
@@ -503,14 +516,14 @@ def tile_visionpermutatorsegmentmixing_kernel(tc, x, g, w, b, ka, gp, wp_bytes, 
         v1_tiles = {}
 
         def combine1(nh, c):
-            view = t_banks["y2", nh, c][:].rearrange("p (x l y) -> p l x y", x=4, l=2)
+            view = t_banks["y2", nh, c][:].rearrange("p (b l a j) -> p l a b j", b=4, l=2, a=4)
             for l in range(2):
                 k = 4 * c + 2 * nh + l
                 t = work.tile([P, 16, 16], F32, name="v1", bufs=16)
                 v1_tiles[c, 2 * nh + l] = t
                 nc.scalar.activation(
-                    out=t[:].rearrange("p i j -> p (i j)").rearrange("p (x y) -> p x y", x=4),
-                    in_=view[:, l, :, :],
+                    out=t[:].rearrange("p (a b) j -> p a b j", a=4),
+                    in_=view[:, l, :, :, :],
                     func=ACT.Identity,
                     scale=amp[:, 2, k : k + 1],
                     bias=a2b2[:, c, 2 * nh + l : 2 * nh + l + 1],
@@ -522,7 +535,7 @@ def tile_visionpermutatorsegmentmixing_kernel(tc, x, g, w, b, ka, gp, wp_bytes, 
             for c in chunks:
                 k = 4 * c + n
                 if nh == 0:
-                    in0 = y01[0][0][:, rows, 4 * (c % 2) + 2 * (c // 2) + l, :]
+                    in0 = y0m[:, rows, 4 * (c % 2) + 2 * (c // 2) + l, :]
                 else:
                     in0 = y0s[:, 2 * (c % 2) + c // 2, rows, 16 * l : 16 * l + 16]
                 nc.vector.scalar_tensor_tensor(
@@ -535,11 +548,12 @@ def tile_visionpermutatorsegmentmixing_kernel(tc, x, g, w, b, ka, gp, wp_bytes, 
                 )
             for c in chunks:
                 k = 4 * c + n
+                a = slice(0, 4) if h is None else slice(2 * h, 2 * h + 2)
                 nc.vector.scalar_tensor_tensor(
-                    out=f_sb[:, c, n, :].rearrange("p (i j) -> p i j", i=16)[:, rows, :],
-                    in0=y01[1][nh][:, :, 4 * (c % 2) + 2 * (c // 2) + l, rows].rearrange("p j i -> p i j"),
+                    out=f_sb[:, c, n, :].rearrange("p (a r) -> p r a", a=4)[:, :, a],
+                    in0=y1[nh][:, :, :, 4 * (c % 2) + 2 * (c // 2) + l, a].rearrange("p b j a -> p (b j) a"),
                     scalar=amp[:, 1, k : k + 1],
-                    in1=v1_tiles[c, n][:, rows, :],
+                    in1=v1_tiles[c, n][:].rearrange("p i j -> p (i j)").rearrange("p (a r) -> p r a", a=4)[:, :, a],
                     op0=MULT,
                     op1=ADD,
                 )
@@ -557,22 +571,29 @@ def tile_visionpermutatorsegmentmixing_kernel(tc, x, g, w, b, ka, gp, wp_bytes, 
             f_tiles["a", n, h] = ft
 
         def f_turn_b(n, h):
-            ps = tr_bank("tb%d_%d" % (n, h), F32, 256)
+            ps = bank("tb%d_%d" % (n, h), F32, 256)
             words = f_tiles["a", n, h][:].bitcast(F32)
             for v in range(2):
-                nc.tensor.transpose(ps[:, 128 * v : 128 * v + 128], words[:, v::2], ident[:])
-            fg = work.tile([P, 512], BF16, name="fg", align_bytes=64)
+                nc.tensor.transpose(ps[:, 128 * v : 128 * v + 128], words[:, v::2], perm_f[:])
+            if n not in f_tiles:
+                fg = work.tile([P, 1024], BF16, name="fg", align_bytes=64)
+                f_tiles[n] = fg
             nc.scalar.copy(
-                out=fg[:].bitcast(F32).rearrange("p (c u) -> p c u", u=2), in_=ps[:].rearrange("p (u c) -> p c u", u=2)
+                out=f_tiles[n][:].bitcast(F32).rearrange("p (b g c u) -> p g b c u", b=4, g=2, u=2)[:, h, :, :, :],
+                in_=ps[:].rearrange("p (u b c) -> p b c u", u=2, b=4),
             )
-            f_tiles[n, h] = fg
+
+        def f_quant(n):
+            f_codes = work.tile([P, 256], U32, name="f_codes", align_bytes=64)
+            f_scales = work.tile([P, 256], U8, name="f_scales", align_bytes=64)
+            nc.vector.quantize_mx(out=f_codes[:].bitcast(FP8X4), scales=f_scales[:], in_=f_tiles[n][:])
+            f_tiles["q", n] = (f_codes, f_scales)
 
         def f_project(n, h, eng="s"):
-            f_codes = work.tile([P, 128], U32, name="f_codes", align_bytes=64)
-            f_scales = work.tile([P, 128], U8, name="f_scales", align_bytes=64)
-            nc.vector.quantize_mx(out=f_codes[:].bitcast(FP8X4), scales=f_scales[:], in_=f_tiles[n, h][:])
-            po = pa_bank("po%d_%d" % (n, h))
-            mx_raw(po[:], f_codes[:], f_scales[:], w_codes[3][:], w_scales[3][:], True, True)
+            f_codes, f_scales = f_tiles["q", n]
+            cols = slice(128 * h, 128 * h + 128)
+            po = bank("po%d_%d" % (n, h))
+            mx_raw(po[:], f_codes[:, cols], f_scales[:, cols], w_codes[3][:], w_scales[3][:], True, True)
             res = work.tile([P, 512], F32, name="res", bufs=4)
             if eng == "s":
                 nc.scalar.copy(out=res[:], in_=po[:])
@@ -581,171 +602,175 @@ def tile_visionpermutatorsegmentmixing_kernel(tc, x, g, w, b, ka, gp, wp_bytes, 
             nc.sync.dma_start(out=out[n].rearrange("i j c -> (i j) c")[128 * h : 128 * h + 128, :], in_=res[:])
 
         with tc.manual_schedule():
-            gain(1, 0, 0)
-            gain(1, 1, 0)
             gain(1, 3, 0)
             gain(1, 2, 0)
-            gain(1, 1, 1)
-            turn(1, 1)
+            gain(1, 1, 0)
+            gain(1, 0, 0)
             gain(1, 3, 1)
-            gain(1, 2, 1)
             turn(1, 3)
-            evac(1, 3)
-            w_inter(1, "v", 1)
+            gain(1, 2, 1)
+            gain(1, 1, 1)
             gain(1, 0, 1)
             gain(2, 1)
-            turn(1, 0)
-            turn(1, 2)
             gain(2, 0)
             w_inter(1, "v", 0)
-            turn(2, 1)
-            evac(1, 2)
-            turn(2, 0)
             gain(2, 2)
-            gain(2, 3)
-            w_quant(1)
-            turn(2, 3)
-            evac(1, 1)
-            gain(0, 2)
-            evac(1, 0)
-            evac(2, 1)
-            gain(0, 0)
-            evac(2, 0)
+            w_inter(1, "v", 1)
             small_vectors()
-            evac(2, 3)
-            gain(0, 3)
-            gain(0, 1)
-            quant_u(1, 1)
-            turn(2, 2)
-            quant_u(1, 0)
-            w_inter(2, "s", 0)
-            w_inter(2, "s", 1)
-            turn(0, 2)
-            turn(0, 0)
-            turn(0, 3)
-            turn(0, 1)
-            quant_u(2, 0)
-            evac(2, 2)
-            pool_mm(1, 1)
-            evac(0, 2)
-            pool_mm(1, 0)
-            pad_moves(1)
-            evac(0, 3)
-            quant_u(2, 1)
-            w_inter(0, "s", 0)
-            w_quant(2)
-            pool_red(1, 1)
-            w_inter(0, "v", 1)
-            evac(0, 0)
-            evac(0, 1)
-            y_both(1, 3)
-            wp_widen(1)
-            y_both(1, 1)
-            w_quant(0)
-            y_both(1, 0)
-            quant_u(0, 0)
-            pool2_mm(0)
-            quant_u(0, 1)
-            pool_mm(0, 0)
-            pool_mm(0, 1)
-            wp_widen(3)
-            pool_red(1, 0)
-            pad_moves(0)
-            pool2_out(0)
-            pool_red(0, 1)
-            pool2_mm(1)
-            wp_widen(0)
-            pool_red(0, 0)
-            swap_mm(3)
-            swap_mm(2)
+            turn(2, 0)
             bias_mean()
-            swap_out(2)
-            y_mm(0, 0, 1)
-            pool2_out(1)
-            swap_mm(1)
-            pool01_sum()
-            swap_out(3)
-            pool2_sum()
-            wp_widen(2)
-            softmax(0)
-            y_mm(0, 0, 3)
-            w_inter(3, "s", 1)
-            swap_out(1)
-            softmax(1)
-            swap_mm(0)
-            y_out(0, 0, 3)
-            softmax(2)
-            y_out(0, 0, 1)
-            softmax(3)
-            y_mm(0, 0, 0)
-            y2_mm(0, 0)
-            softmax(4)
-            y_mm(0, 0, 2)
-            w_inter(3, "s", 0)
-            y_mm(1, 0, 3)
-            swap_bias(1)
-            y2_mm(0, 1)
-            softmax(5)
-            y_mm(1, 0, 2)
-            softmax(6)
-            y_out(0, 0, 0)
-            softmax(7)
-            combine1(0, 0)
-            y_out(0, 0, 2)
-            combine1(0, 1)
-            y_out(1, 0, 2)
-            swap_bias(2)
-            w_quant(3)
-            swap_out(0)
-            y_out(1, 0, 3)
+            w_quant(1)
+            gain(2, 3)
+            evac(2, 0)
+            turn(1, 2)
+            turn(1, 0)
+            evac(1, 3)
+            gain(0, 2)
+            turn(1, 1)
+            gain(0, 0)
+            turn(2, 1)
+            gain(0, 1)
+            turn(2, 2)
+            evac(1, 0)
+            turn(2, 3)
+            turn(0, 2)
+            evac(2, 1)
+            evac(1, 1)
+            gain(0, 3)
+            evac(1, 2)
+            turn(0, 0)
+            quant_u(1, 1)
+            turn(0, 1)
+            pad_moves(1)
+            turn(0, 3)
+            pool_mm(1, 1)
+            quant_u(1, 0)
+            evac(0, 1)
+            evac(2, 2)
+            evac(2, 3)
+            w_inter(0, "v", 0)
+            evac(0, 2)
+            w_inter(2, "s", 0)
+            w_inter(0, "v", 1)
+            evac(0, 3)
+            evac(0, 0)
+            quant_u(2, 0)
             y_both(1, 2)
-            swap_bias(0)
+            w_quant(0)
+            pad_moves(0)
+            w_inter(2, "s", 1)
+            quant_u(0, 1)
+            pool_red(1, 1)
+            y_both(1, 0)
+            quant_u(2, 1)
+            w_quant(2)
+            y_both(1, 1)
+            pool_mm(1, 0)
+            quant_u(0, 0)
+            y_both(1, 3)
+            pool_mm(0, 1)
+            pool_red(0, 1)
+            pool2_mm(0)
+            pool_mm(0, 0)
+            wp_widen(0)
+            pool_red(1, 0)
+            pool_red(0, 0)
+            wp_widen(2)
+            pool2_mm(1)
+            swap_mm(3)
+            swap_mm(1)
+            pool2_out(0)
+            pool01_sum()
+            pool2_out(1)
+            pool2_sum()
+            softmax(0)
+            wp_widen(3)
+            wp_widen(1)
+            swap_out(1)
+            y_mm(0, 0, 2)
+            y_mm(0, 0, 0)
+            softmax(1)
+            swap_out(3)
+            swap_mm(0)
+            softmax(2)
+            y_out(0, 0, 2)
+            w_inter(3, "s", 1)
+            y_mm(0, 0, 3)
+            softmax(3)
+            y_mm(1, 0, 2)
+            y_mm(0, 0, 1)
+            y2_mm(0, 3)
+            softmax(4)
             y2_mm(0, 2)
             swap_bias(3)
-            y2_mm(0, 3)
-            y2_mm(1, 3)
-            y2_mm(1, 2)
+            w_inter(3, "s", 0)
+            softmax(5)
+            y_out(0, 0, 0)
+            swap_mm(2)
+            swap_bias(1)
+            w_quant(3)
+            softmax(6)
+            y_out(1, 0, 2)
+            swap_out(0)
+            y_mm(1, 0, 3)
+            y_out(0, 0, 3)
+            y2_mm(0, 0)
+            softmax(7)
             y_mm(1, 1, 3)
-            combine1(0, 2)
-            combine23(1, (0, 1))
-            y2_mm(1, 0)
-            combine23(0, (0, 1))
+            y2_mm(0, 1)
+            y_out(0, 0, 1)
             combine1(0, 3)
-            combine23(0, (2, 3))
-            combine1(1, 3)
-            combine1(1, 2)
+            y2_mm(1, 3)
             y_mm(1, 1, 2)
-            y2_mm(1, 1)
+            combine1(0, 2)
+            y_out(1, 0, 3)
+            combine1(0, 0)
             y_out(1, 1, 3)
-            combine23(1, (2, 3))
-            combine1(1, 0)
+            combine1(0, 1)
+            swap_bias(0)
+            y2_mm(1, 0)
+            swap_out(2)
+            combine1(1, 3)
+            swap_bias(2)
+            y2_mm(1, 2)
+            y2_mm(1, 1)
+            combine23(0, (2, 3))
             y_out(1, 1, 2)
-            f_turn_a(0, 1)
-            f_turn_a(0, 0)
+            combine23(1, (2, 3))
+            combine23(0, (0, 1))
+            combine1(1, 0)
             combine1(1, 1)
+            combine23(1, (0, 1))
+            f_turn_a(0, 1)
+            combine1(1, 2)
+            f_turn_a(0, 0)
+            combine23(2, (0, 1))
             f_turn_a(1, 1)
-            combine23(2, (2, 3))
-            combine23(3, (0, 1, 2, 3), 1)
             f_turn_a(1, 0)
             f_turn_b(0, 1)
             f_turn_b(0, 0)
+            combine23(2, (2, 3))
+            f_turn_a(2, 0)
+            combine23(3, (0, 1, 2, 3), 1)
+            f_turn_a(2, 1)
             f_turn_b(1, 0)
             f_turn_b(1, 1)
+            f_turn_b(2, 0)
+            f_quant(0)
+            combine23(3, (0, 1, 2, 3), 0)
+            f_turn_b(2, 1)
+            f_project(0, 0)
+            f_quant(2)
             f_turn_a(3, 1)
             f_project(0, 1)
-            f_project(0, 0)
-            combine23(3, (0, 1, 2, 3), 0)
-            f_turn_b(3, 1)
-            f_turn_a(3, 0)
-            f_project(1, 1)
-            f_project(1, 0)
-            f_turn_b(3, 0)
-            combine23(2, (0, 1))
-            f_turn_a(2, 1)
-            f_turn_a(2, 0)
-            f_project(3, 1, "v")
-            f_turn_b(2, 1)
-            f_turn_b(2, 0)
-            f_project(3, 0, "s")
+            f_quant(1)
             f_project(2, 1)
             f_project(2, 0)
+            f_turn_a(3, 0)
+            f_turn_b(3, 1)
+            f_turn_b(3, 0)
+            f_quant(3)
+            f_project(1, 0)
+            f_project(1, 1)
+            f_project(3, 1, "v")
+            f_project(3, 0, "s")

@@ -15,10 +15,18 @@ MULT = mybir.AluOpType.mult
 MAX = mybir.AluOpType.max
 SUB = mybir.AluOpType.subtract
 AX = mybir.AxisListType.X
-ACT = mybir.ActivationFunctionType
+COPY = mybir.ActivationFunctionType.Copy
+EXP = mybir.ActivationFunctionType.Exp
+IDENTITY = mybir.ActivationFunctionType.Identity
 
 P = 128
-FLOPS = 4 * 2 * 1024 * 512 * 512
+K = 512
+R = 16
+E = 32
+PIXELS = R * R
+GAP = 96
+EDGE = 128
+FLOPS = 4 * 2 * 4 * PIXELS * K * K
 
 
 def tile_visionpermutatorsegmentmixing_kernel(tc, x, g, w, b, ka, gp, wp_bytes, wp_scale, out):
@@ -34,36 +42,36 @@ def tile_visionpermutatorsegmentmixing_kernel(tc, x, g, w, b, ka, gp, wp_bytes, 
         def bank(name, dtype=F32, width=512):
             return psum.tile([P, width], dtype, name=name, tag="bank", bufs=8)
 
-        tr_bank = ym_bank = mm_bank = pa_bank = bank
-
-        pad_codes = [sb([P, 96 + 16 * 128], U32, "pad_codes%d" % m) for m in range(2)]
-        pad_scales = [[sb([P, 768], U8, "pad_scales%d_%d" % (m, k)) for k in range(2)] for m in range(2)]
-        w_codes = [sb([P, 512], U32, "w_codes%d" % m) for m in range(4)]
+        spread_codes = [sb([P, GAP + R * P], U32, "spread_codes%d" % m) for m in range(2)]
+        spread_scales = [
+            [sb([P, EDGE + K + EDGE], U8, "spread_scales%d_%d" % (m, shift)) for shift in range(2)] for m in range(2)
+        ]
+        w_codes = [sb([P, K], U32, "w_codes%d" % m) for m in range(4)]
         w_scales = [
-            pad_scales[m][0][:, 128:640] if m < 2 else sb([P, 512], U8, "w_scales%d" % m)[:] for m in range(4)
+            spread_scales[m][0][:, EDGE : EDGE + K] if m < 2 else sb([P, K], U8, "w_scales%d" % m)[:] for m in range(4)
         ]
 
         ident = sb([P, P], F32, "ident")
         make_identity(nc, ident[:])
-        g_row = sb([P, 3, 512], BF16, "g_row")
-        nc.vector.memset(g_row[:], 0.0)
-        nc.sync.dma_start(out=g_row[0:1, :, :], in_=g.rearrange("(o m) k -> o m k", o=1))
+        gain_row = sb([P, 3, K], BF16, "gain_row")
+        nc.vector.memset(gain_row[:], 0.0)
+        nc.sync.dma_start(out=gain_row[0:1, :, :], in_=g.rearrange("(o m) k -> o m k", o=1))
         ones = sb([P, P], BF16, "ones")
         nc.vector.memset(ones[:], 1.0)
         small = sb([P, P], BF16, "small")
         nc.vector.memset(small[:], 0.0)
 
-        x_tok = x.rearrange("n i j c -> (n i j) c").rearrange("(t p) c -> p t c", p=P)
-        x2 = sb([P, 8, 512], BF16, "x2")
-        x0 = sb([P, 16, 256], BF16, "x0")
-        x1 = sb([P, 16, 256], BF16, "x1")
-        w_raw = [sb([P, 4, 512], BF16, "w_raw%d" % m) for m in range(3)]
+        x2 = sb([P, 8, K], BF16, "x2")
+        x0 = sb([P, R, 256], BF16, "x0")
+        x1 = sb([P, R, 256], BF16, "x1")
+        w_raw = [sb([P, 4, K], BF16, "w_raw%d" % m) for m in range(3)]
+        tokens = x.rearrange("n i j c -> (n i j) c").rearrange("(t p) c -> p t c", p=P)
 
-        def load_x2(h):
-            nc.sync.dma_start(out=x2[:, 4 * h : 4 * h + 4, :], in_=x_tok[:, 4 * h : 4 * h + 4, :])
+        def load_x2(part):
+            nc.sync.dma_start(out=x2[:, 4 * part : 4 * part + 4, :], in_=tokens[:, 4 * part : 4 * part + 4, :])
 
         def load_w(m):
-            nc.sync.dma_start(out=w_raw[m][:], in_=w[m].rearrange("(p j) n -> p j n", j=4))
+            nc.sync.dma_start(out=w_raw[m][:], in_=w[m].rearrange("(p t) n -> p t n", t=4))
 
         for part in range(2):
             for h in range(2):
@@ -77,19 +85,20 @@ def tile_visionpermutatorsegmentmixing_kernel(tc, x, g, w, b, ka, gp, wp_bytes, 
         load_x2(1)
         nc.sync.dma_start(
             out=small[0:32, :].rearrange("r (q e) -> r q e", q=4),
-            in_=b[0:2, :].rearrange("m (i e) -> (m i) e", e=32).unsqueeze(1).to_broadcast([32, 4, 32]),
+            in_=b[0:2, :].rearrange("m (z e) -> (m z) e", e=E).unsqueeze(1).to_broadcast([32, 4, E]),
         )
         nc.sync.dma_start(out=small[32:36, :], in_=b[2:3, :].rearrange("o (c x) -> (o c) x", x=P))
-        nc.sync.dma_start(out=small[36:48, :], in_=ka.rearrange("m (c x) -> (m c) x", x=P))
+        for m in range(3):
+            nc.sync.dma_start(out=small[36 + 4 * m : 40 + 4 * m, :], in_=ka[m].rearrange("(c x) -> c x", x=P))
         nc.sync.dma_start(out=small[48:52, :], in_=gp.rearrange("(c x) -> c x", x=P))
         for n in range(4):
             nc.sync.dma_start(out=x0[n : P : 4, :, :], in_=x[n].rearrange("i j (h c) -> (j h) i c", h=2))
         load_w(0)
         load_w(2)
-        wp_codes = sb([P, 4, 512], U8, "wp_codes")
-        nc.sync.dma_start(out=wp_codes[:], in_=wp_bytes.rearrange("(p j) n -> p j n", j=4))
-        wp_s = sb([P, 4], F32, "wp_s")
-        nc.sync.dma_start(out=wp_s[:], in_=wp_scale.rearrange("(p j) o -> p (j o)", j=4))
+        wp_in = sb([P, 4, K], U8, "wp_in")
+        nc.sync.dma_start(out=wp_in[:], in_=wp_bytes.rearrange("(p t) n -> p t n", t=4))
+        wp_row_scale = sb([P, 4], F32, "wp_row_scale")
+        nc.sync.dma_start(out=wp_row_scale[:], in_=wp_scale.rearrange("(p t) o -> p (t o)", t=4))
 
         ident_bf = sb([P, P], BF16, "ident_bf")
         nc.vector.tensor_copy(out=ident_bf[:], in_=ident[:])
@@ -108,669 +117,674 @@ def tile_visionpermutatorsegmentmixing_kernel(tc, x, g, w, b, ka, gp, wp_bytes, 
             out=perm1[:].rearrange("p (h y) -> p h y", h=2),
             in_=ident[:].rearrange("p (y h) -> p h y", h=2),
         )
-        e_sum = sb([P, 32], F32, "e_sum")
-        nc.vector.tensor_reduce(out=e_sum[:], in_=ident[:].rearrange("p (a e) -> p e a", e=32), axis=AX, op=ADD)
-        e_sel = sb([P, 4, P], F32, "e_sel")
-        nc.vector.memset(e_sel[:], 0.0)
-        for q in range(4):
-            nc.vector.tensor_scalar(
-                out=e_sel[:, q, 32 * q : 32 * q + 32], in0=e_sum[:], scalar1=1.0 / 256.0, scalar2=None, op0=MULT
-            )
-        l_mask = sb([P, 2], F32, "l_mask")
-        nc.vector.tensor_reduce(out=l_mask[:], in_=ident[:].rearrange("p (l y) -> p l y", l=2), axis=AX, op=ADD)
-        nc.vector.tensor_scalar(out=l_mask[:], in0=l_mask[:], scalar1=1.0 / 256.0, scalar2=None, op0=MULT)
+        perm = [perm0, perm1, ident]
+        same_e = sb([P, E], F32, "same_e")
+        nc.vector.tensor_reduce(out=same_e[:], in_=ident[:].rearrange("p (a e) -> p e a", e=E), axis=AX, op=ADD)
+        sum_e = sb([P, P], F32, "sum_e")
+        nc.vector.tensor_scalar(
+            out=sum_e[:].rearrange("p (q e) -> p q e", q=4),
+            in0=same_e[:].unsqueeze(1).to_broadcast([P, 4, E]),
+            scalar1=1.0 / PIXELS,
+            scalar2=None,
+            op0=MULT,
+        )
+        in_quadrant = sb([P, 4], F32, "in_quadrant")
+        nc.vector.tensor_reduce(out=in_quadrant[:], in_=ident[:].rearrange("p (q e) -> p q e", q=4), axis=AX, op=ADD)
+        in_image = sb([P, 2], F32, "in_image")
+        nc.vector.tensor_reduce(out=in_image[:], in_=ident[:].rearrange("p (l y) -> p l y", l=2), axis=AX, op=ADD)
+        nc.vector.tensor_scalar(out=in_image[:], in0=in_image[:], scalar1=1.0 / PIXELS, scalar2=None, op0=MULT)
         for m in (1, 0):
-            for k in range(2):
-                nc.vector.memset(pad_scales[m][k][:].bitcast(I32), 0)
-            pad_engine = nc.vector if m == 1 else nc.gpsimd
-            pad_engine.memset(pad_codes[m][:].bitcast(I32), 0)
-        warm = sb([P, 1], F32, "warm")
-        nc.scalar.activation(out=warm[:], in_=e_sum[:, 0:1], func=ACT.Exp)
+            for shift in range(2):
+                nc.vector.memset(spread_scales[m][shift][:].bitcast(I32), 0)
+            filler = nc.vector if m == 1 else nc.gpsimd
+            filler.memset(spread_codes[m][:].bitcast(I32), 0)
+        table = sb([P, 1], F32, "table")
+        nc.scalar.activation(out=table[:], in_=same_e[:, 0:1], func=EXP)
 
-        gains = sb([P, 3, 512], BF16, "gains")
+        gains = sb([P, 3, K], BF16, "gains")
         for m in (1, 2, 0):
-            g_ps = tr_bank("g_ps%d" % m)
-            nc.tensor.matmul(g_ps[:], lhsT=ones[:], rhs=g_row[:, m, :], start=True, stop=True)
-            nc.scalar.copy(out=gains[:, m, :], in_=g_ps[:])
+            ps = bank("gains_ps%d" % m)
+            nc.tensor.matmul(ps[:], lhsT=ones[:], rhs=gain_row[:, m, :], start=True, stop=True)
+            nc.scalar.copy(out=gains[:, m, :], in_=ps[:])
 
         vec = sb([P, 52], F32, "vec")
 
         def small_vectors():
-            sm_ps = tr_bank("sm_ps", BF16)
-            nc.tensor.transpose(sm_ps[:, 0:P], small[:], ident_bf[:])
-            nc.scalar.copy(out=vec[:], in_=sm_ps[:, 0:52])
+            ps = bank("small_ps", BF16)
+            nc.tensor.transpose(ps[:, 0:P], small[:], ident_bf[:])
+            nc.scalar.copy(out=vec[:], in_=ps[:, 0:52])
 
-        grouped = [sb([P, 4096], BF16, "grouped%d" % m) for m in range(3)]
+        u_grouped = [sb([P, 4 * 1024], BF16, "u_grouped%d" % m) for m in range(3)]
         u_codes = [sb([P, 1024], U32, "u_codes%d" % m) for m in range(3)]
         u_scales = [sb([P, 1024], U8, "u_scales%d" % m) for m in range(3)]
-        u = [keep.tile([P, 8, 512], BF16, name="u%d" % m, tag="u%d" % m, align_bytes=64) for m in range(2)] + [x2]
-        xs = [x0, x1, x2]
-        perms = [perm0, perm1, ident]
-        t_banks = {}
-        full = slice(0, 512)
+        u = [keep.tile([P, 8, K], BF16, name="u%d" % m, tag="u%d" % m, align_bytes=64) for m in range(2)] + [x2]
+        banks = {}
 
-        def gain(m, q, part=None):
-            z = slice(0, 16) if part is None else slice(8 * part, 8 * part + 8)
+        def scale(m, k, part=None):
             if m == 2:
                 nc.vector.tensor_tensor(
-                    out=u[2][:, 2 * q : 2 * q + 2, :],
-                    in0=x2[:, 2 * q : 2 * q + 2, :],
-                    in1=gains[:, 2, :].unsqueeze(1).to_broadcast([P, 2, 512]),
+                    out=u[2][:, 2 * k : 2 * k + 2, :],
+                    in0=x2[:, 2 * k : 2 * k + 2, :],
+                    in1=gains[:, 2, :].unsqueeze(1).to_broadcast([P, 2, K]),
                     op=MULT,
                 )
-            else:
-                size = z.stop - z.start
-                gain_z = gains[:, m, :].rearrange("p (z e) -> p z e", e=32)[:, z, :]
-                nc.vector.tensor_tensor(
-                    out=u[m][:, 2 * q : 2 * q + 2, :].rearrange("p s (z e) -> p s z e", e=32)[:, :, z, :],
-                    in0=xs[m][:].rearrange("p z (s e) -> p s z e", e=32)[:, q:8:4, z, :],
-                    in1=gain_z.unsqueeze(1).to_broadcast([P, 2, size, 32]),
-                    op=MULT,
-                )
+                return
+            z = slice(0, R) if part is None else slice(8 * part, 8 * part + 8)
+            gain = gains[:, m, :].rearrange("p (z e) -> p z e", e=E)[:, z, :]
+            nc.vector.tensor_tensor(
+                out=u[m][:, 2 * k : 2 * k + 2, :].rearrange("p s (z e) -> p s z e", e=E)[:, :, z, :],
+                in0=(x0, x1)[m][:].rearrange("p z (s e) -> p s z e", e=E)[:, k:8:4, z, :],
+                in1=gain.unsqueeze(1).to_broadcast([P, 2, z.stop - z.start, E]),
+                op=MULT,
+            )
 
-        def turn(m, q):
-            ps = tr_bank("t%d_%d" % (m, q))
-            t_banks[m, q] = ps
-            view = ps[:].rearrange("p (u t c) -> p u t c", t=2, u=2)
+        def turn(m, k):
+            ps = bank("turn%d_%d" % (m, k))
+            banks["turn", m, k] = ps
+            view = ps[:].rearrange("p (v r c) -> p v r c", v=2, r=2)
             words = u[m][:].bitcast(F32)
-            for t in range(2):
+            for r in range(2):
                 for v in range(2):
-                    nc.tensor.transpose(view[:, v, t, :], words[:, 2 * q + t, v::2], perms[m][:])
+                    nc.tensor.transpose(view[:, v, r, :], words[:, 2 * k + r, v::2], perm[m][:])
 
-        def evac(m, q):
-            ps = t_banks[m, q]
-            words = grouped[m][:].bitcast(F32)
-            if m < 2:
-                src = ps[:].rearrange("p (u f h n c) -> p n (f h) c u", u=2, f=2, h=2, n=2)
-                for n in range(2):
-                    if m == 1:
-                        dst = words[:, 512 * q + 256 * n : 512 * q + 256 * n + 256]
-                    elif n == 0:
-                        dst = words[:, 256 * q : 256 * q + 256]
-                    if m == 0 and n == 1:
-                        dst = words[:, 1024:].rearrange("p (k q c u) -> p q k c u", k=4, q=4, u=2)[:, q, :, :, :]
-                    else:
-                        dst = dst.rearrange("p (k c u) -> p k c u", k=4, u=2)
-                    nc.scalar.copy(out=dst, in_=src[:, n, :, :, :])
-            else:
+        def collect(m, k):
+            ps = banks["turn", m, k]
+            words = u_grouped[m][:].bitcast(F32)
+            if m == 2:
                 nc.scalar.copy(
-                    out=words.rearrange("p (n x l y u) -> p n l x y u", n=2, x=4, l=2, u=2)[:, q // 2, q % 2, :, :, :],
-                    in_=ps[:].rearrange("p (u x y) -> p x y u", u=2, x=4),
+                    out=words.rearrange("p (n b l y v) -> p n l b y v", n=2, b=4, l=2, v=2)[:, k // 2, k % 2, :, :, :],
+                    in_=ps[:].rearrange("p (v b y) -> p b y v", v=2, b=4),
                 )
+                return
+            src = ps[:].rearrange("p (v f h n y) -> p n (f h) y v", v=2, f=2, h=2, n=2)
+            for half in range(2):
+                if m == 0 and half == 1:
+                    dst = words[:, 1024:].rearrange("p (k q y v) -> p q k y v", k=4, q=4, v=2)[:, k, :, :, :]
+                else:
+                    start = 512 * k + 256 * half if m == 1 else 256 * k
+                    dst = words[:, start : start + 256].rearrange("p (k y v) -> p k y v", k=4, v=2)
+                nc.scalar.copy(out=dst, in_=src[:, half, :, :, :])
 
-        def quant_u(m, half):
-            cols = slice(512 * half, 512 * half + 512)
+        def quantise_u(m, part):
+            cols = slice(512 * part, 512 * part + 512)
             nc.vector.quantize_mx(
                 out=u_codes[m][:, cols].bitcast(FP8X4),
                 scales=u_scales[m][:, cols],
-                in_=grouped[m][:, 2048 * half : 2048 * half + 2048],
+                in_=u_grouped[m][:, 2048 * part : 2048 * part + 2048],
             )
 
-        w_groups = [sb([P, 512, 4], BF16, "w_grouped%d" % m) for m in range(3)]
-        w_groups.append(w_groups[0])
+        w_grouped = [sb([P, K, 4], BF16, "w_grouped%d" % m) for m in range(3)]
+        w_grouped.append(w_grouped[0])
 
-        def w_inter(m, eng, h, parts=2):
-            n = 512 // parts
-            src = (w_raw + [wp_w])[m]
-            dst = w_groups[m][:, n * h : n * h + n, :]
+        def interleave_w(m, part, copy):
+            dst = w_grouped[m][:, 256 * part : 256 * part + 256, :]
+            src = wp_wide[:] if m == 3 else w_raw[m][:]
             if m == 0:
-                dst = dst.rearrange("p (a b e) j -> p a b e j", a=2, b=4)
-                src = src.rearrange("p j (b a e) -> p a b e j", a=4, b=4)[:, 2 * h : 2 * h + 2, :, :, :]
+                dst = dst.rearrange("p (a b e) t -> p a b e t", a=2, b=4)
+                src = src.rearrange("p t (b a e) -> p a b e t", a=4, b=4)[:, 2 * part : 2 * part + 2, :, :, :]
             else:
-                src = src[:, :, n * h : n * h + n].rearrange("p j n -> p n j")
-            if eng == "s":
-                nc.scalar.copy(out=dst, in_=src)
-            elif eng == "v":
-                nc.vector.tensor_copy(out=dst, in_=src)
-            else:
-                nc.gpsimd.tensor_scalar(out=dst, in0=src, scalar1=1.0, scalar2=0.0, op0=MULT, op1=ADD)
+                src = src[:, :, 256 * part : 256 * part + 256].rearrange("p t n -> p n t")
+            copy(out=dst, in_=src)
 
-        def w_quant(m):
+        def quantise_w(m):
             nc.vector.quantize_mx(
                 out=w_codes[m][:].bitcast(FP8X4),
-                scales=w_scales[m][:],
-                in_=w_groups[m][:].rearrange("p n j -> p (n j)"),
+                scales=w_scales[m],
+                in_=w_grouped[m][:].rearrange("p n t -> p (n t)"),
             )
 
-        def mx_raw(o, lc, ls, rc, rs, start, stop):
+        def multiply(dst, lhs, lhs_scale, rhs, rhs_scale, start=True, stop=True):
             nc.tensor.matmul_mx(
-                out=o, lhsT=lc.bitcast(FP8X4), lhsT_scale=ls, rhs=rc.bitcast(FP8X4), rhs_scale=rs, start=start, stop=stop
+                out=dst,
+                lhsT=lhs.bitcast(FP8X4),
+                lhsT_scale=lhs_scale,
+                rhs=rhs.bitcast(FP8X4),
+                rhs_scale=rhs_scale,
+                start=start,
+                stop=stop,
             )
 
-        def mx(o, m, lcols, rcols, w_stationary, start=True, stop=True):
-            u_c, u_s = u_codes[m], u_scales[m]
-            w_c, w_s = w_codes[m], w_scales[m]
-            lc, ls, rc, rs = (w_c, w_s, u_c, u_s) if w_stationary else (u_c, u_s, w_c, w_s)
-            mx_raw(o, lc[:, lcols], ls[:, lcols], rc[:, rcols], rs[:, rcols], start, stop)
+        pooled = [sb([P, 4, 16], F32, "pooled%d" % m) for m in range(2)]
 
-        red = [sb([P, 4, 16], F32, "red%d" % m) for m in range(2)]
+        def pool_products(m, part):
+            ps = bank("pool%d_%d" % (m, part))
+            banks["pool", m, part] = ps
+            cols = slice(512 * part, 512 * part + 512)
+            for k in range(4):
+                group = slice(P * k, P * k + P)
+                multiply(
+                    ps[:],
+                    w_codes[m][:, group],
+                    w_scales[m][:, group],
+                    u_codes[m][:, cols],
+                    u_scales[m][:, cols],
+                    k == 0,
+                    k == 3,
+                )
 
-        def pool_mm(m, half):
-            ps = bank("pa%d_%d" % (m, half))
-            t_banks["pool", m, half] = ps
-            for z in range(4):
-                mx(ps[:], m, slice(128 * z, 128 * z + 128), slice(512 * half, 512 * half + 512), True, z == 0, z == 3)
-
-        def pool_red(m, half):
-            ps = t_banks["pool", m, half]
+        def pool_reduce(m, part):
+            ps = banks["pool", m, part]
             if m == 1:
-                dst = red[1][:, 2 * half : 2 * half + 2, :]
-                src = ps[:].rearrange("p (q k y) -> p q k y", q=2, y=16)
-            elif half == 0:
-                dst = red[0][:, :, 0:8]
-                src = ps[:].rearrange("p (q k y) -> p q k y", q=4, y=16)
+                dst = pooled[1][:, 2 * part : 2 * part + 2, :]
+                src = ps[:].rearrange("p (q k y) -> p q k y", q=2, y=R)
+            elif part == 0:
+                dst = pooled[0][:, :, 0:8]
+                src = ps[:].rearrange("p (q k y) -> p q k y", q=4, y=R)
             else:
-                dst = red[0][:].rearrange("p q (n k l) -> p n k q l", n=2, l=2)[:, 1, :, :, :]
+                dst = pooled[0][:].rearrange("p q (n k l) -> p n k q l", n=2, l=2)[:, 1, :, :, :]
                 src = ps[:].rearrange("p (k q l y) -> p k q l y", k=4, q=4, l=2)
             nc.vector.tensor_reduce(out=dst, in_=src, axis=AX, op=ADD)
 
-        pb_sb = sb([P, 2, 512], F32, "pb_sb")
+        pooled2 = sb([P, 2, K], F32, "pooled2")
 
-        def pool2_mm(n):
-            ps = pa_bank("pb%d" % n)
-            for t in range(4):
-                c0 = 512 * n + 128 * t
-                mx(ps[:], 2, slice(c0, c0 + 128), full, False, t == 0, t == 3)
-            t_banks["pb", n] = ps
+        def pool2_products(half):
+            ps = bank("pool2_%d" % half)
+            for k in range(4):
+                rows = slice(512 * half + P * k, 512 * half + P * k + P)
+                multiply(
+                    ps[:],
+                    u_codes[2][:, rows],
+                    u_scales[2][:, rows],
+                    w_codes[2][:, 0:K],
+                    w_scales[2][:, 0:K],
+                    k == 0,
+                    k == 3,
+                )
+            banks["pool2", half] = ps
 
-        def pool2_out(n):
-            nc.scalar.copy(out=pb_sb[:, n, :], in_=t_banks["pb", n][:])
+        def pool2_copy(half):
+            nc.scalar.copy(out=pooled2[:, half, :], in_=banks["pool2", half][:])
 
-        def pad_moves(m):
+        def spread_w(m):
             nc.vector.tensor_copy(
-                out=pad_codes[m][:, 96:].rearrange("p (z c) -> p z c", c=128)[:, :, 0:32].bitcast(I32),
-                in_=w_codes[m][:].rearrange("p (z e) -> p z e", e=32).bitcast(I32),
+                out=spread_codes[m][:, GAP:].rearrange("p (z c) -> p z c", c=P)[:, :, 0:E].bitcast(I32),
+                in_=w_codes[m][:].rearrange("p (z e) -> p z e", e=E).bitcast(I32),
             )
             nc.vector.tensor_copy(
-                out=pad_scales[m][1][:, 160:672].bitcast(I32), in_=pad_scales[m][0][:, 128:640].bitcast(I32)
+                out=spread_scales[m][1][:, EDGE + E : EDGE + E + K].bitcast(I32),
+                in_=spread_scales[m][0][:, EDGE : EDGE + K].bitcast(I32),
             )
 
-        y0m = sb([P, 16, 8, 16], F32, "y0m")
-        y1 = [sb([P, 4, 16, 8, 4], F32, "y1_%d" % n) for n in range(2)]
+        y0_half0 = sb([P, R, 8, R], F32, "y0_half0")
+        y1 = [sb([P, 4, R, 8, 4], F32, "y1_%d" % half) for half in range(2)]
+        y0_half1 = sb([P, 4, R, 32], F32, "y0_half1")
 
-        def y_dst(m, nh, z):
+        def y_place(m, half, z):
             if m == 0:
-                return y0m[:, z, :, :].rearrange("p k (b a) -> p k b a", b=4)
-            return y1[nh][:, :, z, :, :].rearrange("p b k a -> p k b a")
+                return y0_half0[:, z, :, :].rearrange("p k (b a) -> p k b a", b=4)
+            return y1[half][:, :, z, :, :].rearrange("p b k a -> p k b a")
 
-        def y_bias(m, z):
-            i = 4 * (z % 4) + z // 4 if m == 0 else 16 + z
+        def bias_of(m, z):
+            i = 4 * (z % 4) + z // 4 if m == 0 else R + z
             return vec[:, i : i + 1]
-        y0s = sb([P, 4, 16, 32], F32, "y0s")
 
-        def swap_mm(k):
-            ps = bank("ys%d" % k)
-            t_banks["ys", k] = ps
-            mx(ps[:], 0, slice(512 + 128 * k, 640 + 128 * k), full, False)
+        def add_bias(m, half, z, ps):
+            nc.scalar.activation(
+                out=y_place(m, half, z),
+                in_=ps.rearrange("p (k b a) -> p k b a", k=8, b=4),
+                func=IDENTITY,
+                bias=bias_of(m, z),
+            )
 
-        def swap_out(k):
-            nc.vector.transpose(out=y0s[:, k, :, :].rearrange("p z r -> p (z r)"), in_=t_banks["ys", k][:])
+        def masked_passes(dst, m, z, columns):
+            for q in range(4):
+                shift = (z - q) % 2
+                code = GAP + P * z - E * q
+                scale_col = EDGE + E * (z - q + shift)
+                cols = columns(q)
+                multiply(
+                    dst,
+                    spread_codes[m][:, code : code + P],
+                    spread_scales[m][shift][:, scale_col : scale_col + P],
+                    u_codes[m][:, cols],
+                    u_scales[m][:, cols],
+                    q == 0,
+                    q == 3,
+                )
 
-        def swap_bias(k):
+        def quadrant_product(k):
+            ps = bank("quadrant%d" % k)
+            banks["quadrant", k] = ps
+            rows = slice(512 + P * k, 512 + P * k + P)
+            multiply(ps[:], u_codes[0][:, rows], u_scales[0][:, rows], w_codes[0][:, 0:K], w_scales[0][:, 0:K])
+
+        def quadrant_turn(k):
+            nc.vector.transpose(out=y0_half1[:, k, :, :].rearrange("p z r -> p (z r)"), in_=banks["quadrant", k][:])
+
+        def quadrant_bias(k):
             nc.vector.tensor_tensor(
-                out=y0s[:, k, :, :].rearrange("p (a b) r -> p a b r", a=4),
-                in0=y0s[:, k, :, :].rearrange("p (a b) r -> p a b r", a=4),
-                in1=vec[:, 0:16].rearrange("p (b a) -> p a b", b=4).unsqueeze(3).to_broadcast([P, 4, 4, 32]),
+                out=y0_half1[:, k, :, :].rearrange("p (a b) r -> p a b r", a=4),
+                in0=y0_half1[:, k, :, :].rearrange("p (a b) r -> p a b r", a=4),
+                in1=vec[:, 0:R].rearrange("p (b a) -> p a b", b=4).unsqueeze(3).to_broadcast([P, 4, 4, 32]),
                 op=ADD,
             )
 
-        def y_mm(m, nh, quad):
-            ps = bank("ym%d_%d_%d" % (m, nh, quad))
-            t_banks["y", m, nh, quad] = ps
-            for d in range(4):
-                z = 4 * quad + d
-                for q in range(4):
-                    c0 = 256 * q + 128 * nh if m == 1 else 128 * q
-                    cols = slice(c0, c0 + 128)
-                    start = 96 + 128 * z - 32 * q
-                    odd = (z - q) % 2
-                    s_start = 128 + 32 * (z - q + odd)
-                    mx_raw(
-                        ps[:, 128 * d : 128 * d + 128],
-                        pad_codes[m][:, start : start + 128],
-                        pad_scales[m][odd][:, s_start : s_start + 128],
-                        u_codes[m][:, cols],
-                        u_scales[m][:, cols],
-                        q == 0,
-                        q == 3,
-                    )
+        def masked(m, half, k):
+            ps = bank("masked%d_%d_%d" % (m, half, k))
+            banks["masked", m, half, k] = ps
 
-        def y_out(m, nh, quad):
-            ps = t_banks["y", m, nh, quad]
-            for d in range(4):
-                z = 4 * quad + d
-                nc.scalar.activation(
-                    out=y_dst(m, nh, z),
-                    in_=ps[:, 128 * d : 128 * d + 128].rearrange("p (k b a) -> p k b a", k=8, b=4),
-                    func=ACT.Identity,
-                    bias=y_bias(m, z),
-                )
+            def columns(q):
+                start = 256 * q + P * half if m == 1 else P * q
+                return slice(start, start + P)
 
-        def y_both(m, pair):
-            ps = bank("yb%d_%d" % (m, pair))
+            for d in range(4):
+                masked_passes(ps[:, P * d : P * d + P], m, 4 * k + d, columns)
+
+        def masked_out(m, half, k):
+            for d in range(4):
+                add_bias(m, half, 4 * k + d, banks["masked", m, half, k][:, P * d : P * d + P])
+
+        def masked_both_halves(k):
+            ps = bank("masked_both%d" % k)
             for d in range(2):
-                z = 2 * pair + d
-                for q in range(4):
-                    cols = slice(256 * q, 256 * q + 256)
-                    start = 96 + 128 * z - 32 * q
-                    odd = (z - q) % 2
-                    s_start = 128 + 32 * (z - q + odd)
-                    mx_raw(
-                        ps[:, 256 * d : 256 * d + 256],
-                        pad_codes[m][:, start : start + 128],
-                        pad_scales[m][odd][:, s_start : s_start + 128],
-                        u_codes[m][:, cols],
-                        u_scales[m][:, cols],
-                        q == 0,
-                        q == 3,
-                    )
-            for n in range(2):
+                masked_passes(ps[:, 256 * d : 256 * d + 256], 1, 2 * k + d, lambda q: slice(256 * q, 256 * q + 256))
+            for half in range(2):
                 for d in range(2):
-                    z = 2 * pair + d
-                    nc.scalar.activation(
-                        out=y_dst(m, n, z),
-                        in_=ps[:, 256 * d + 128 * n : 256 * d + 128 * n + 128].rearrange(
-                            "p (k b a) -> p k b a", k=8, b=4
-                        ),
-                        func=ACT.Identity,
-                        bias=y_bias(m, z),
-                    )
+                    start = 256 * d + P * half
+                    add_bias(1, half, 2 * k + d, ps[:, start : start + P])
 
         b_mean = sb([P, 1], F32, "b_mean")
         b_pool = sb([P, 4], F32, "b_pool")
 
-        def bias_mean():
+        def mean_bias():
             nc.vector.tensor_reduce(out=b_mean[:], in_=vec[:, 0:32], axis=AX, op=ADD)
             nc.vector.scalar_tensor_tensor(
                 out=b_pool[:],
                 in0=b_mean[:].to_broadcast([P, 4]),
-                scalar=1.0 / 16.0,
+                scalar=1.0 / R,
                 in1=vec[:, 32:36],
                 op0=MULT,
                 op1=ADD,
             )
 
+        wp_wide = sb([P, 4, K], BF16, "wp_wide")
 
-        wp_w = sb([P, 4, 512], BF16, "wp_w")
-
-        def wp_widen(j):
+        def widen_wp(t):
             nc.scalar.activation(
-                out=wp_w[:, j, :], in_=wp_codes[:, j, :].bitcast(E4M3), func=ACT.Copy, scale=wp_s[:, j : j + 1]
+                out=wp_wide[:, t, :], in_=wp_in[:, t, :].bitcast(E4M3), func=COPY, scale=wp_row_scale[:, t : t + 1]
             )
 
-        amp = sb([P, 3, 16], F32, "amp")
-        a2b2 = sb([P, 4, 4], F32, "a2b2")
+        weight = sb([P, 3, 16], F32, "weight")
+        weight_b2 = sb([P, 4, 4], F32, "weight_b2")
+        step_tile = {}
 
-        chain = {}
-
-        def pool2_sum():
-            p2_ps = bank("p2_ps")
+        def pool2_finish():
+            ps = bank("pool2_ps")
             for c in range(4):
-                for n in range(2):
-                    k = 4 * c + 2 * n
+                for half in range(2):
+                    k = 4 * c + 2 * half
                     nc.tensor.matmul(
-                        p2_ps[:, k : k + 2],
-                        lhsT=pb_sb[:, n, 128 * c : 128 * c + 128],
-                        rhs=l_mask[:],
+                        ps[:, k : k + 2],
+                        lhsT=pooled2[:, half, P * c : P * c + P],
+                        rhs=in_image[:],
                         start=True,
                         stop=True,
                     )
-            pool_a = sb([P, 4, 4], F32, "pool_a")
+            part2 = sb([P, 4, 4], F32, "part2")
             nc.vector.tensor_tensor(
-                out=pool_a[:],
-                in0=p2_ps[:, 0:16].rearrange("p (c n) -> p c n", c=4),
+                out=part2[:],
+                in0=ps[:, 0:16].rearrange("p (c n) -> p c n", c=4),
                 in1=b_pool[:].unsqueeze(2).to_broadcast([P, 4, 4]),
                 op=ADD,
             )
-            chain["pool_a"] = pool_a
+            step_tile["part2"] = part2
 
-        def pool01_sum():
-            sel_ps = bank("sel_ps")
+        def pool01_finish():
+            ps = bank("pool01_ps")
             for m in range(2):
-                for q in range(4):
-                    nc.tensor.matmul(
-                        sel_ps[:, 0:16],
-                        lhsT=e_sel[:, q, :],
-                        rhs=red[m][:, q, :],
-                        start=(m == 0 and q == 0),
-                        stop=(m == 1 and q == 3),
-                    )
-            chain["sel"] = sel_ps
+                nc.tensor.matmul(
+                    ps[:, 0:64],
+                    lhsT=sum_e[:],
+                    rhs=pooled[m][:].rearrange("p q k -> p (q k)"),
+                    start=(m == 0),
+                    stop=(m == 1),
+                )
+            picked = sb([P, 4, 16], F32, "picked")
+            nc.vector.tensor_tensor(
+                out=picked[:],
+                in0=ps[:, 0:64].rearrange("p (q k) -> p q k", q=4),
+                in1=in_quadrant[:].unsqueeze(2).to_broadcast([P, 4, 16]),
+                op=MULT,
+            )
+            part01 = sb([P, 16], F32, "part01")
+            nc.vector.tensor_reduce(out=part01[:], in_=picked[:].rearrange("p q k -> p k q"), axis=AX, op=ADD)
+            step_tile["part01"] = part01
 
         def softmax(step):
             if step == 0:
                 pool = sb([P, 4, 4], F32, "pool")
-                for n in range(2):
+                part01 = step_tile["part01"][:].rearrange("p (n f h l) -> p n f h l", n=2, f=2, h=2)
+                part2 = step_tile["part2"][:].rearrange("p (h f) (n l) -> p n f h l", h=2, n=2)
+                for half in range(2):
                     nc.vector.tensor_tensor(
-                        out=pool[:].rearrange("p (h f) (n l) -> p n f h l", h=2, n=2)[:, n, :, :, :],
-                        in0=chain["sel"][:, 0:16].rearrange("p (n f h l) -> p n f h l", n=2, f=2, h=2)[:, n, :, :, :],
-                        in1=chain["pool_a"][:].rearrange("p (h f) (n l) -> p n f h l", h=2, n=2)[:, n, :, :, :],
+                        out=pool[:].rearrange("p (h f) (n l) -> p n f h l", h=2, n=2)[:, half, :, :, :],
+                        in0=part01[:, half, :, :, :],
+                        in1=part2[:, half, :, :, :],
                         op=ADD,
                     )
-                chain["pool"] = pool
+                step_tile["pool"] = pool
             elif step == 1:
                 logit = sb([P, 3, 16], F32, "logit")
                 nc.vector.tensor_tensor(
                     out=logit[:].rearrange("p m (c n) -> p m c n", c=4),
-                    in0=chain["pool"][:].unsqueeze(1).to_broadcast([P, 3, 4, 4]),
+                    in0=step_tile["pool"][:].unsqueeze(1).to_broadcast([P, 3, 4, 4]),
                     in1=vec[:, 36:48].rearrange("p (m c) -> p m c", m=3).unsqueeze(3).to_broadcast([P, 3, 4, 4]),
                     op=MULT,
                 )
-                chain["logit"] = logit
+                step_tile["logit"] = logit
             elif step == 2:
-                l_max = sb([P, 16], F32, "l_max")
+                largest = sb([P, 16], F32, "largest")
                 nc.vector.tensor_reduce(
-                    out=l_max[:], in_=chain["logit"][:].rearrange("p m k -> p k m"), axis=AX, op=MAX
+                    out=largest[:], in_=step_tile["logit"][:].rearrange("p m k -> p k m"), axis=AX, op=MAX
                 )
-                chain["max"] = l_max
+                step_tile["largest"] = largest
             elif step == 3:
                 shifted = sb([P, 3, 16], F32, "shifted")
                 nc.vector.tensor_tensor(
                     out=shifted[:],
-                    in0=chain["logit"][:],
-                    in1=chain["max"][:].unsqueeze(1).to_broadcast([P, 3, 16]),
+                    in0=step_tile["logit"][:],
+                    in1=step_tile["largest"][:].unsqueeze(1).to_broadcast([P, 3, 16]),
                     op=SUB,
                 )
                 expo = sb([P, 3, 16], F32, "expo")
-                nc.scalar.activation(out=expo[:], in_=shifted[:], func=ACT.Exp)
-                chain["expo"] = expo
+                nc.scalar.activation(out=expo[:], in_=shifted[:], func=EXP)
+                step_tile["expo"] = expo
             elif step == 4:
-                e_tot = sb([P, 16], F32, "e_tot")
+                total = sb([P, 16], F32, "total")
                 nc.vector.tensor_reduce(
-                    out=e_tot[:], in_=chain["expo"][:].rearrange("p m k -> p k m"), axis=AX, op=ADD
+                    out=total[:], in_=step_tile["expo"][:].rearrange("p m k -> p k m"), axis=AX, op=ADD
                 )
-                e_gp = sb([P, 3, 4, 4], F32, "e_gp")
+                expo_gp = sb([P, 3, 4, 4], F32, "expo_gp")
                 nc.vector.tensor_tensor(
-                    out=e_gp[:],
-                    in0=chain["expo"][:].rearrange("p m (c n) -> p m c n", c=4),
+                    out=expo_gp[:],
+                    in0=step_tile["expo"][:].rearrange("p m (c n) -> p m c n", c=4),
                     in1=vec[:, 48:52].unsqueeze(1).unsqueeze(3).to_broadcast([P, 3, 4, 4]),
                     op=MULT,
                 )
-                chain["tot"], chain["gp"] = e_tot, e_gp
+                step_tile["total"], step_tile["expo_gp"] = total, expo_gp
             elif step == 5:
-                e_inv = sb([P, 16], F32, "e_inv")
-                nc.vector.reciprocal(out=e_inv[:], in_=chain["tot"][:])
-                chain["inv"] = e_inv
+                inverse = sb([P, 16], F32, "inverse")
+                nc.vector.reciprocal(out=inverse[:], in_=step_tile["total"][:])
+                step_tile["inverse"] = inverse
             elif step == 6:
                 nc.vector.tensor_tensor(
-                    out=amp[:],
-                    in0=chain["gp"][:].rearrange("p m c n -> p m (c n)"),
-                    in1=chain["inv"][:].unsqueeze(1).to_broadcast([P, 3, 16]),
+                    out=weight[:],
+                    in0=step_tile["expo_gp"][:].rearrange("p m c n -> p m (c n)"),
+                    in1=step_tile["inverse"][:].unsqueeze(1).to_broadcast([P, 3, 16]),
                     op=MULT,
                 )
             else:
                 nc.vector.tensor_tensor(
-                    out=a2b2[:],
-                    in0=amp[:, 2, :].rearrange("p (c n) -> p c n", c=4),
+                    out=weight_b2[:],
+                    in0=weight[:, 2, :].rearrange("p (c n) -> p c n", c=4),
                     in1=vec[:, 32:36].unsqueeze(2).to_broadcast([P, 4, 4]),
                     op=MULT,
                 )
 
-        f_sb = keep.tile([P, 4, 4, 256], BF16, name="f_sb", tag="u0", align_bytes=64)
+        f_sum = keep.tile([P, 4, 4, PIXELS], BF16, name="f_sum", tag="u0", align_bytes=64)
+        partial = {}
 
-        def y2_mm(nh, c):
-            ps = mm_bank("y2_%d_%d" % (nh, c))
-            t_banks["y2", nh, c] = ps
-            mx(ps[:], 2, slice(128 * c, 128 * c + 128), slice(512 * nh, 512 * nh + 512), True)
+        def branch2(half, c):
+            ps = bank("y2_%d_%d" % (half, c))
+            banks["y2", half, c] = ps
+            chunk = slice(P * c, P * c + P)
+            cols = slice(512 * half, 512 * half + 512)
+            multiply(ps[:], w_codes[2][:, chunk], w_scales[2][:, chunk], u_codes[2][:, cols], u_scales[2][:, cols])
 
-        v1_tiles = {}
-
-        def combine1(nh, c):
-            view = t_banks["y2", nh, c][:].rearrange("p (b l a j) -> p l a b j", b=4, l=2, a=4)
+        def weigh2(half, c):
+            view = banks["y2", half, c][:].rearrange("p (b l a j) -> p l a b j", b=4, l=2, a=4)
             for l in range(2):
-                k = 4 * c + 2 * nh + l
-                t = work.tile([P, 16, 16], F32, name="v1", bufs=16)
-                v1_tiles[c, 2 * nh + l] = t
+                n = 2 * half + l
+                k = 4 * c + n
+                part = work.tile([P, R, R], F32, name="part", bufs=16)
+                partial[c, n] = part
                 nc.scalar.activation(
-                    out=t[:].rearrange("p (a b) j -> p a b j", a=4),
+                    out=part[:].rearrange("p (a b) j -> p a b j", a=4),
                     in_=view[:, l, :, :, :],
-                    func=ACT.Identity,
-                    scale=amp[:, 2, k : k + 1],
-                    bias=a2b2[:, c, 2 * nh + l : 2 * nh + l + 1],
+                    func=IDENTITY,
+                    scale=weight[:, 2, k : k + 1],
+                    bias=weight_b2[:, c, n : n + 1],
                 )
 
-        def combine23(n, chunks, h=None):
-            nh, l = n // 2, n % 2
-            rows = slice(0, 16) if h is None else slice(8 * h, 8 * h + 8)
+        def weigh01(n, chunks, part=None):
+            half, l = n // 2, n % 2
+            a = slice(0, 4) if part is None else slice(2 * part, 2 * part + 2)
+            rows = slice(4 * a.start, 4 * a.stop)
             for c in chunks:
                 k = 4 * c + n
-                if nh == 0:
-                    in0 = y0m[:, rows, 4 * (c % 2) + 2 * (c // 2) + l, :]
+                group = 2 * (c % 2) + c // 2
+                if half == 0:
+                    y0 = y0_half0[:, rows, 2 * group + l, :]
                 else:
-                    in0 = y0s[:, 2 * (c % 2) + c // 2, rows, 16 * l : 16 * l + 16]
+                    y0 = y0_half1[:, group, rows, R * l : R * l + R]
                 nc.vector.scalar_tensor_tensor(
-                    out=v1_tiles[c, n][:, rows, :],
-                    in0=in0,
-                    scalar=amp[:, 0, k : k + 1],
-                    in1=v1_tiles[c, n][:, rows, :],
+                    out=partial[c, n][:, rows, :],
+                    in0=y0,
+                    scalar=weight[:, 0, k : k + 1],
+                    in1=partial[c, n][:, rows, :],
                     op0=MULT,
                     op1=ADD,
                 )
             for c in chunks:
                 k = 4 * c + n
-                a = slice(0, 4) if h is None else slice(2 * h, 2 * h + 2)
+                group = 2 * (c % 2) + c // 2
+                so_far = partial[c, n][:].rearrange("p i j -> p (i j)")
                 nc.vector.scalar_tensor_tensor(
-                    out=f_sb[:, c, n, :].rearrange("p (a r) -> p r a", a=4)[:, :, a],
-                    in0=y1[nh][:, :, :, 4 * (c % 2) + 2 * (c // 2) + l, a].rearrange("p b j a -> p (b j) a"),
-                    scalar=amp[:, 1, k : k + 1],
-                    in1=v1_tiles[c, n][:].rearrange("p i j -> p (i j)").rearrange("p (a r) -> p r a", a=4)[:, :, a],
+                    out=f_sum[:, c, n, :].rearrange("p (a r) -> p r a", a=4)[:, :, a],
+                    in0=y1[half][:, :, :, 2 * group + l, a].rearrange("p b j a -> p (b j) a"),
+                    scalar=weight[:, 1, k : k + 1],
+                    in1=so_far.rearrange("p (a r) -> p r a", a=4)[:, :, a],
                     op0=MULT,
                     op1=ADD,
                 )
 
-        f_tiles = {}
+        f_rows, f_grouped, f_quantised = {}, {}, {}
 
-        def f_turn_a(n, h):
-            ps = ym_bank("ta%d_%d" % (n, h), BF16, 512)
+        def f_to_tokens(n, part):
+            ps = bank("f_rows%d_%d" % (n, part), BF16, 512)
             for c in range(4):
                 nc.tensor.transpose(
-                    ps[:, 128 * c : 128 * c + 128], f_sb[:, c, n, 128 * h : 128 * h + 128], ident_bf[:]
+                    ps[:, P * c : P * c + P], f_sum[:, c, n, P * part : P * part + P], ident_bf[:]
                 )
-            ft = work.tile([P, 512], BF16, name="ft")
-            nc.scalar.copy(out=ft[:], in_=ps[:])
-            f_tiles["a", n, h] = ft
+            rows = work.tile([P, K], BF16, name="rows")
+            nc.scalar.copy(out=rows[:], in_=ps[:])
+            f_rows[n, part] = rows
 
-        def f_turn_b(n, h):
-            ps = bank("tb%d_%d" % (n, h), F32, 256)
-            words = f_tiles["a", n, h][:].bitcast(F32)
+        def f_to_channels(n, part):
+            ps = bank("f_words%d_%d" % (n, part), F32, 256)
+            words = f_rows[n, part][:].bitcast(F32)
             for v in range(2):
-                nc.tensor.transpose(ps[:, 128 * v : 128 * v + 128], words[:, v::2], perm_f[:])
-            if n not in f_tiles:
-                fg = work.tile([P, 1024], BF16, name="fg", align_bytes=64)
-                f_tiles[n] = fg
+                nc.tensor.transpose(ps[:, P * v : P * v + P], words[:, v::2], perm_f[:])
+            if n not in f_grouped:
+                grouped = work.tile([P, 4 * PIXELS], BF16, name="grouped", align_bytes=64)
+                f_grouped[n] = grouped
             nc.scalar.copy(
-                out=f_tiles[n][:].bitcast(F32).rearrange("p (b g c u) -> p g b c u", b=4, g=2, u=2)[:, h, :, :, :],
-                in_=ps[:].rearrange("p (u b c) -> p b c u", u=2, b=4),
+                out=f_grouped[n][:].bitcast(F32).rearrange("p (b g c v) -> p g b c v", b=4, g=2, v=2)[:, part, :, :, :],
+                in_=ps[:].rearrange("p (v b c) -> p b c v", v=2, b=4),
             )
 
-        def f_quant(n):
-            f_codes = work.tile([P, 256], U32, name="f_codes", align_bytes=64)
-            f_scales = work.tile([P, 256], U8, name="f_scales", align_bytes=64)
-            nc.vector.quantize_mx(out=f_codes[:].bitcast(FP8X4), scales=f_scales[:], in_=f_tiles[n][:])
-            f_tiles["q", n] = (f_codes, f_scales)
+        def quantise_f(n):
+            codes = work.tile([P, PIXELS], U32, name="codes", align_bytes=64)
+            scales = work.tile([P, PIXELS], U8, name="scales", align_bytes=64)
+            nc.vector.quantize_mx(out=codes[:].bitcast(FP8X4), scales=scales[:], in_=f_grouped[n][:])
+            f_quantised[n] = (codes, scales)
 
-        def f_project(n, h, eng="s"):
-            f_codes, f_scales = f_tiles["q", n]
-            cols = slice(128 * h, 128 * h + 128)
-            po = bank("po%d_%d" % (n, h))
-            mx_raw(po[:], f_codes[:, cols], f_scales[:, cols], w_codes[3][:], w_scales[3][:], True, True)
-            res = work.tile([P, 512], F32, name="res", bufs=4)
-            if eng == "s":
-                nc.scalar.copy(out=res[:], in_=po[:])
-            else:
-                nc.vector.tensor_copy(out=res[:], in_=po[:])
-            nc.sync.dma_start(out=out[n].rearrange("i j c -> (i j) c")[128 * h : 128 * h + 128, :], in_=res[:])
+        def project(n, part, copy):
+            codes, scales = f_quantised[n]
+            rows = slice(P * part, P * part + P)
+            ps = bank("project%d_%d" % (n, part))
+            multiply(ps[:], codes[:, rows], scales[:, rows], w_codes[3][:, 0:K], w_scales[3][:, 0:K])
+            result = work.tile([P, K], F32, name="result", bufs=4)
+            copy(out=result[:], in_=ps[:])
+            nc.sync.dma_start(out=out[n].rearrange("i j c -> (i j) c")[rows, :], in_=result[:])
 
         with tc.manual_schedule():
-            gain(1, 3, 0)
-            gain(1, 2, 0)
-            gain(1, 1, 0)
-            gain(1, 0, 0)
-            gain(1, 3, 1)
+            for k in (1, 3, 0, 2):
+                scale(1, k, 0)
+            for k in (1, 3):
+                scale(1, k, 1)
             turn(1, 3)
-            gain(1, 2, 1)
-            gain(1, 1, 1)
-            gain(1, 0, 1)
-            gain(2, 1)
-            gain(2, 0)
-            w_inter(1, "v", 0)
-            gain(2, 2)
-            w_inter(1, "v", 1)
-            small_vectors()
-            turn(2, 0)
-            bias_mean()
-            w_quant(1)
-            gain(2, 3)
-            evac(2, 0)
-            turn(1, 2)
+            scale(1, 2, 1)
+            for k in (2, 1):
+                turn(1, k)
+            interleave_w(1, 1, nc.vector.tensor_copy)
+            scale(1, 0, 1)
             turn(1, 0)
-            evac(1, 3)
-            gain(0, 2)
-            turn(1, 1)
-            gain(0, 0)
-            turn(2, 1)
-            gain(0, 1)
+            collect(1, 2)
+            interleave_w(1, 0, nc.vector.tensor_copy)
+            collect(1, 1)
+            for k in range(2):
+                scale(2, k)
+            collect(1, 3)
+            scale(2, 2)
+            quantise_w(1)
+            scale(2, 3)
+            quantise_u(1, 1)
+            spread_w(1)
+            turn(2, 0)
+            small_vectors()
             turn(2, 2)
-            evac(1, 0)
+            for k in (0, 3):
+                scale(0, k)
+            turn(2, 1)
+            collect(2, 2)
             turn(2, 3)
-            turn(0, 2)
-            evac(2, 1)
-            evac(1, 1)
-            gain(0, 3)
-            evac(1, 2)
+            for k in (2, 1):
+                collect(k, 0)
+            collect(2, 1)
+            pool_products(1, 1)
+            collect(2, 3)
             turn(0, 0)
-            quant_u(1, 1)
-            turn(0, 1)
-            pad_moves(1)
+            for k in (2, 1):
+                scale(0, k)
             turn(0, 3)
-            pool_mm(1, 1)
-            quant_u(1, 0)
-            evac(0, 1)
-            evac(2, 2)
-            evac(2, 3)
-            w_inter(0, "v", 0)
-            evac(0, 2)
-            w_inter(2, "s", 0)
-            w_inter(0, "v", 1)
-            evac(0, 3)
-            evac(0, 0)
-            quant_u(2, 0)
-            y_both(1, 2)
-            w_quant(0)
-            pad_moves(0)
-            w_inter(2, "s", 1)
-            quant_u(0, 1)
-            pool_red(1, 1)
-            y_both(1, 0)
-            quant_u(2, 1)
-            w_quant(2)
-            y_both(1, 1)
-            pool_mm(1, 0)
-            quant_u(0, 0)
-            y_both(1, 3)
-            pool_mm(0, 1)
-            pool_red(0, 1)
-            pool2_mm(0)
-            pool_mm(0, 0)
-            wp_widen(0)
-            pool_red(1, 0)
-            pool_red(0, 0)
-            wp_widen(2)
-            pool2_mm(1)
-            swap_mm(3)
-            swap_mm(1)
-            pool2_out(0)
-            pool01_sum()
-            pool2_out(1)
-            pool2_sum()
+            quantise_u(1, 0)
+            for k in (2, 1):
+                turn(0, k)
+            interleave_w(2, 0, nc.scalar.copy)
+            pool_reduce(1, 1)
+            collect(0, 3)
+            interleave_w(0, 1, nc.vector.tensor_copy)
+            masked(1, 0, 2)
+            interleave_w(2, 1, nc.scalar.copy)
+            interleave_w(0, 0, nc.vector.tensor_copy)
+            quantise_w(2)
+            for k in range(2):
+                quantise_u(2, k)
+            collect(0, 2)
+            widen_wp(3)
+            for k in (1, 0):
+                collect(0, k)
+            masked_both_halves(2)
+            quantise_w(0)
+            masked_both_halves(3)
+            pool_products(1, 0)
+            masked_out(1, 0, 2)
+            quantise_u(0, 1)
+            spread_w(0)
+            pool_reduce(1, 0)
+            masked(1, 0, 3)
+            masked_out(1, 0, 3)
+            quadrant_product(2)
+            pool2_products(1)
+            quantise_u(0, 0)
+            pool_products(0, 1)
+            widen_wp(2)
+            masked_both_halves(1)
+            pool_reduce(0, 1)
+            pool_products(0, 0)
+            widen_wp(0)
+            masked(0, 0, 2)
+            pool_reduce(0, 0)
+            quadrant_product(3)
+            mean_bias()
+            quadrant_turn(2)
+            pool2_products(0)
+            pool2_copy(1)
+            quadrant_product(1)
+            widen_wp(1)
+            branch2(1, 1)
+            pool2_copy(0)
+            pool01_finish()
+            quadrant_turn(3)
+            pool2_finish()
             softmax(0)
-            wp_widen(3)
-            wp_widen(1)
-            swap_out(1)
-            y_mm(0, 0, 2)
-            y_mm(0, 0, 0)
+            interleave_w(3, 0, nc.scalar.copy)
             softmax(1)
-            swap_out(3)
-            swap_mm(0)
+            masked_out(0, 0, 2)
             softmax(2)
-            y_out(0, 0, 2)
-            w_inter(3, "s", 1)
-            y_mm(0, 0, 3)
+            interleave_w(3, 1, nc.scalar.copy)
+            masked(0, 0, 3)
+            quadrant_product(0)
+            masked_out(0, 0, 3)
             softmax(3)
-            y_mm(1, 0, 2)
-            y_mm(0, 0, 1)
-            y2_mm(0, 3)
+            quadrant_turn(1)
+            branch2(0, 0)
             softmax(4)
-            y2_mm(0, 2)
-            swap_bias(3)
-            w_inter(3, "s", 0)
-            softmax(5)
-            y_out(0, 0, 0)
-            swap_mm(2)
-            swap_bias(1)
-            w_quant(3)
-            softmax(6)
-            y_out(1, 0, 2)
-            swap_out(0)
-            y_mm(1, 0, 3)
-            y_out(0, 0, 3)
-            y2_mm(0, 0)
-            softmax(7)
-            y_mm(1, 1, 3)
-            y2_mm(0, 1)
-            y_out(0, 0, 1)
-            combine1(0, 3)
-            y2_mm(1, 3)
-            y_mm(1, 1, 2)
-            combine1(0, 2)
-            y_out(1, 0, 3)
-            combine1(0, 0)
-            y_out(1, 1, 3)
-            combine1(0, 1)
-            swap_bias(0)
-            y2_mm(1, 0)
-            swap_out(2)
-            combine1(1, 3)
-            swap_bias(2)
-            y2_mm(1, 2)
-            y2_mm(1, 1)
-            combine23(0, (2, 3))
-            y_out(1, 1, 2)
-            combine23(1, (2, 3))
-            combine23(0, (0, 1))
-            combine1(1, 0)
-            combine1(1, 1)
-            combine23(1, (0, 1))
-            f_turn_a(0, 1)
-            combine1(1, 2)
-            f_turn_a(0, 0)
-            combine23(2, (0, 1))
-            f_turn_a(1, 1)
-            f_turn_a(1, 0)
-            f_turn_b(0, 1)
-            f_turn_b(0, 0)
-            combine23(2, (2, 3))
-            f_turn_a(2, 0)
-            combine23(3, (0, 1, 2, 3), 1)
-            f_turn_a(2, 1)
-            f_turn_b(1, 0)
-            f_turn_b(1, 1)
-            f_turn_b(2, 0)
-            f_quant(0)
-            combine23(3, (0, 1, 2, 3), 0)
-            f_turn_b(2, 1)
-            f_project(0, 0)
-            f_quant(2)
-            f_turn_a(3, 1)
-            f_project(0, 1)
-            f_quant(1)
-            f_project(2, 1)
-            f_project(2, 0)
-            f_turn_a(3, 0)
-            f_turn_b(3, 1)
-            f_turn_b(3, 0)
-            f_quant(3)
-            f_project(1, 0)
-            f_project(1, 1)
-            f_project(3, 1, "v")
-            f_project(3, 0, "s")
+            for k in range(2):
+                masked(0, 0, k)
+            quadrant_bias(1)
+            masked_out(0, 0, 0)
+            for k in range(5, 8):
+                softmax(k)
+            weigh2(1, 1)
+            branch2(0, 1)
+            quadrant_turn(0)
+            weigh2(0, 0)
+            masked_out(0, 0, 1)
+            weigh2(0, 1)
+            masked_both_halves(0)
+            branch2(0, 3)
+            branch2(1, 0)
+            for k in (3, 2):
+                quadrant_bias(k)
+            branch2(0, 2)
+            for k in (3, 2):
+                weigh2(0, k)
+            quadrant_bias(0)
+            branch2(1, 3)
+            quantise_w(3)
+            branch2(1, 2)
+            weigh01(0, (0, 1))
+            masked(1, 1, 2)
+            weigh2(1, 2)
+            masked(1, 1, 3)
+            weigh01(1, (0, 1))
+            weigh01(0, (2, 3))
+            weigh2(1, 0)
+            masked_out(1, 1, 2)
+            weigh2(1, 3)
+            masked_out(1, 1, 3)
+            f_to_tokens(0, 0)
+            weigh01(1, (2, 3))
+            for k in range(2):
+                f_to_tokens(k, 1)
+            weigh01(2, (0, 1))
+            f_to_tokens(1, 0)
+            for k in range(2):
+                f_to_channels(0, k)
+            for k in (1, 0):
+                f_to_channels(1, k)
+            weigh01(2, (2, 3))
+            quantise_f(0)
+            for k in range(2):
+                f_to_tokens(2, k)
+            quantise_f(1)
+            for k in range(2):
+                project(k, 0, nc.scalar.copy)
+            f_to_channels(2, 1)
+            for k in (1, 0):
+                project(k, 1, nc.scalar.copy)
+            weigh01(3, (0, 1, 2, 3), 0)
+            f_to_channels(2, 0)
+            f_to_tokens(3, 0)
+            weigh01(3, (0, 1, 2, 3), 1)
+            f_to_tokens(3, 1)
+            f_to_channels(3, 0)
+            quantise_f(2)
+            f_to_channels(3, 1)
+            project(2, 0, nc.scalar.copy)
+            quantise_f(3)
+            project(2, 1, nc.scalar.copy)
+            project(3, 1, nc.vector.tensor_copy)
+            project(3, 0, nc.scalar.copy)

from contextlib import ExitStack

import concourse.mybir as mybir
from concourse.masks import make_identity

F32 = mybir.dt.float32
BF16 = mybir.dt.bfloat16
U32 = mybir.dt.uint32
I32 = mybir.dt.int32
U8 = mybir.dt.uint8
E4M3 = mybir.dt.float8_e4m3fn
FP8X4 = mybir.dt.float8_e4m3fn_x4
ADD = mybir.AluOpType.add
MULT = mybir.AluOpType.mult
MAX = mybir.AluOpType.max
SUB = mybir.AluOpType.subtract
AX = mybir.AxisListType.X
COPY = mybir.ActivationFunctionType.Copy
EXP = mybir.ActivationFunctionType.Exp
IDENTITY = mybir.ActivationFunctionType.Identity

P = 128
K = 512
R = 16
E = 32
PIXELS = R * R
GAP = 96
EDGE = 128
FLOPS = 4 * 2 * 4 * PIXELS * K * K


def tile_visionpermutatorsegmentmixing_kernel(tc, x, g, w, b, ka, gp, wp_bytes, wp_scale, out):
    nc = tc.nc
    with ExitStack() as ctx:
        keep = ctx.enter_context(tc.tile_pool(name="keep", bufs=1))
        work = ctx.enter_context(tc.tile_pool(name="work", bufs=4))
        psum = ctx.enter_context(tc.psum_pool(name="psum", bufs=2))

        def sb(shape, dtype, name):
            return keep.tile(shape, dtype, name=name, align_bytes=64)

        def bank(name, dtype=F32, width=512):
            return psum.tile([P, width], dtype, name=name, tag="bank", bufs=8)

        spread_codes = [sb([P, GAP + R * P], U32, "spread_codes%d" % m) for m in range(2)]
        spread_scales = [
            [sb([P, EDGE + K + EDGE], U8, "spread_scales%d_%d" % (m, shift)) for shift in range(2)] for m in range(2)
        ]
        w_codes = [sb([P, K], U32, "w_codes%d" % m) for m in range(4)]
        w_scales = [
            spread_scales[m][0][:, EDGE : EDGE + K] if m < 2 else sb([P, K], U8, "w_scales%d" % m)[:] for m in range(4)
        ]

        ident = sb([P, P], F32, "ident")
        make_identity(nc, ident[:])
        gain_row = sb([P, 3, K], BF16, "gain_row")
        nc.vector.memset(gain_row[:], 0.0)
        nc.sync.dma_start(out=gain_row[0:1, :, :], in_=g.rearrange("(o m) k -> o m k", o=1))
        ones = sb([P, P], BF16, "ones")
        nc.vector.memset(ones[:], 1.0)
        small = sb([P, P], BF16, "small")
        nc.vector.memset(small[:], 0.0)

        x2 = sb([P, 8, K], BF16, "x2")
        x0 = sb([P, R, 256], BF16, "x0")
        x1 = sb([P, R, 256], BF16, "x1")
        w_raw = [sb([P, 4, K], BF16, "w_raw%d" % m) for m in range(3)]
        tokens = x.rearrange("n i j c -> (n i j) c").rearrange("(t p) c -> p t c", p=P)

        def load_x2(part):
            nc.sync.dma_start(out=x2[:, 4 * part : 4 * part + 4, :], in_=tokens[:, 4 * part : 4 * part + 4, :])

        def load_w(m):
            nc.sync.dma_start(out=w_raw[m][:], in_=w[m].rearrange("(p t) n -> p t n", t=4))

        for part in range(2):
            for h in range(2):
                j = slice(8 * part, 8 * part + 8)
                nc.sync.dma_start(
                    out=x1[h : P : 2, j, :],
                    in_=x[:, :, j, 256 * h : 256 * h + 256].rearrange("n i j c -> (n i) j c"),
                )
        load_w(1)
        load_x2(0)
        load_x2(1)
        nc.sync.dma_start(
            out=small[0:32, :].rearrange("r (q e) -> r q e", q=4),
            in_=b[0:2, :].rearrange("m (z e) -> (m z) e", e=E).unsqueeze(1).to_broadcast([32, 4, E]),
        )
        nc.sync.dma_start(out=small[32:36, :], in_=b[2:3, :].rearrange("o (c x) -> (o c) x", x=P))
        for m in range(3):
            nc.sync.dma_start(out=small[36 + 4 * m : 40 + 4 * m, :], in_=ka[m].rearrange("(c x) -> c x", x=P))
        nc.sync.dma_start(out=small[48:52, :], in_=gp.rearrange("(c x) -> c x", x=P))
        for n in range(4):
            nc.sync.dma_start(out=x0[n : P : 4, :, :], in_=x[n].rearrange("i j (h c) -> (j h) i c", h=2))
        load_w(0)
        load_w(2)
        wp_in = sb([P, 4, K], U8, "wp_in")
        nc.sync.dma_start(out=wp_in[:], in_=wp_bytes.rearrange("(p t) n -> p t n", t=4))
        wp_row_scale = sb([P, 4], F32, "wp_row_scale")
        nc.sync.dma_start(out=wp_row_scale[:], in_=wp_scale.rearrange("(p t) o -> p (t o)", t=4))

        ident_bf = sb([P, P], BF16, "ident_bf")
        nc.vector.tensor_copy(out=ident_bf[:], in_=ident[:])
        perm0 = sb([P, P], F32, "perm0")
        nc.vector.tensor_copy(
            out=perm0[:].rearrange("p (h n y) -> p h n y", h=2, n=4),
            in_=ident[:].rearrange("p (y h n) -> p h n y", h=2, n=4),
        )
        perm_f = sb([P, P], F32, "perm_f")
        nc.vector.tensor_copy(
            out=perm_f[:].rearrange("p (b a j) -> p b a j", a=2, b=4),
            in_=ident[:].rearrange("p (a b j) -> p b a j", a=2, b=4),
        )
        perm1 = sb([P, P], F32, "perm1")
        nc.vector.tensor_copy(
            out=perm1[:].rearrange("p (h y) -> p h y", h=2),
            in_=ident[:].rearrange("p (y h) -> p h y", h=2),
        )
        perm = [perm0, perm1, ident]
        same_e = sb([P, E], F32, "same_e")
        nc.vector.tensor_reduce(out=same_e[:], in_=ident[:].rearrange("p (a e) -> p e a", e=E), axis=AX, op=ADD)
        sum_e = sb([P, P], F32, "sum_e")
        nc.vector.tensor_scalar(
            out=sum_e[:].rearrange("p (q e) -> p q e", q=4),
            in0=same_e[:].unsqueeze(1).to_broadcast([P, 4, E]),
            scalar1=1.0 / PIXELS,
            scalar2=None,
            op0=MULT,
        )
        in_quadrant = sb([P, 4], F32, "in_quadrant")
        nc.vector.tensor_reduce(out=in_quadrant[:], in_=ident[:].rearrange("p (q e) -> p q e", q=4), axis=AX, op=ADD)
        in_image = sb([P, 2], F32, "in_image")
        nc.vector.tensor_reduce(out=in_image[:], in_=ident[:].rearrange("p (l y) -> p l y", l=2), axis=AX, op=ADD)
        nc.vector.tensor_scalar(out=in_image[:], in0=in_image[:], scalar1=1.0 / PIXELS, scalar2=None, op0=MULT)
        for m in (1, 0):
            for shift in range(2):
                nc.vector.memset(spread_scales[m][shift][:].bitcast(I32), 0)
            filler = nc.vector if m == 1 else nc.gpsimd
            filler.memset(spread_codes[m][:].bitcast(I32), 0)
        table = sb([P, 1], F32, "table")
        nc.scalar.activation(out=table[:], in_=same_e[:, 0:1], func=EXP)

        gains = sb([P, 3, K], BF16, "gains")
        for m in (1, 2, 0):
            ps = bank("gains_ps%d" % m)
            nc.tensor.matmul(ps[:], lhsT=ones[:], rhs=gain_row[:, m, :], start=True, stop=True)
            nc.scalar.copy(out=gains[:, m, :], in_=ps[:])

        vec = sb([P, 52], F32, "vec")

        def small_vectors():
            ps = bank("small_ps", BF16)
            nc.tensor.transpose(ps[:, 0:P], small[:], ident_bf[:])
            nc.scalar.copy(out=vec[:], in_=ps[:, 0:52])

        u_grouped = [sb([P, 4 * 1024], BF16, "u_grouped%d" % m) for m in range(3)]
        u_codes = [sb([P, 1024], U32, "u_codes%d" % m) for m in range(3)]
        u_scales = [sb([P, 1024], U8, "u_scales%d" % m) for m in range(3)]
        u = [keep.tile([P, 8, K], BF16, name="u%d" % m, tag="u%d" % m, align_bytes=64) for m in range(2)] + [x2]
        banks = {}

        def scale(m, k, part=None):
            if m == 2:
                nc.vector.tensor_tensor(
                    out=u[2][:, 2 * k : 2 * k + 2, :],
                    in0=x2[:, 2 * k : 2 * k + 2, :],
                    in1=gains[:, 2, :].unsqueeze(1).to_broadcast([P, 2, K]),
                    op=MULT,
                )
                return
            z = slice(0, R) if part is None else slice(8 * part, 8 * part + 8)
            gain = gains[:, m, :].rearrange("p (z e) -> p z e", e=E)[:, z, :]
            nc.vector.tensor_tensor(
                out=u[m][:, 2 * k : 2 * k + 2, :].rearrange("p s (z e) -> p s z e", e=E)[:, :, z, :],
                in0=(x0, x1)[m][:].rearrange("p z (s e) -> p s z e", e=E)[:, k:8:4, z, :],
                in1=gain.unsqueeze(1).to_broadcast([P, 2, z.stop - z.start, E]),
                op=MULT,
            )

        def turn(m, k):
            ps = bank("turn%d_%d" % (m, k))
            banks["turn", m, k] = ps
            view = ps[:].rearrange("p (v r c) -> p v r c", v=2, r=2)
            words = u[m][:].bitcast(F32)
            for r in range(2):
                for v in range(2):
                    nc.tensor.transpose(view[:, v, r, :], words[:, 2 * k + r, v::2], perm[m][:])

        def collect(m, k):
            ps = banks["turn", m, k]
            words = u_grouped[m][:].bitcast(F32)
            if m == 2:
                nc.scalar.copy(
                    out=words.rearrange("p (n b l y v) -> p n l b y v", n=2, b=4, l=2, v=2)[:, k // 2, k % 2, :, :, :],
                    in_=ps[:].rearrange("p (v b y) -> p b y v", v=2, b=4),
                )
                return
            src = ps[:].rearrange("p (v f h n y) -> p n (f h) y v", v=2, f=2, h=2, n=2)
            for half in range(2):
                if m == 0 and half == 1:
                    dst = words[:, 1024:].rearrange("p (k q y v) -> p q k y v", k=4, q=4, v=2)[:, k, :, :, :]
                else:
                    start = 512 * k + 256 * half if m == 1 else 256 * k
                    dst = words[:, start : start + 256].rearrange("p (k y v) -> p k y v", k=4, v=2)
                nc.scalar.copy(out=dst, in_=src[:, half, :, :, :])

        def quantise_u(m, part):
            cols = slice(512 * part, 512 * part + 512)
            nc.vector.quantize_mx(
                out=u_codes[m][:, cols].bitcast(FP8X4),
                scales=u_scales[m][:, cols],
                in_=u_grouped[m][:, 2048 * part : 2048 * part + 2048],
            )

        w_grouped = [sb([P, K, 4], BF16, "w_grouped%d" % m) for m in range(3)]
        w_grouped.append(w_grouped[0])

        def interleave_w(m, part, copy):
            dst = w_grouped[m][:, 256 * part : 256 * part + 256, :]
            src = wp_wide[:] if m == 3 else w_raw[m][:]
            if m == 0:
                dst = dst.rearrange("p (a b e) t -> p a b e t", a=2, b=4)
                src = src.rearrange("p t (b a e) -> p a b e t", a=4, b=4)[:, 2 * part : 2 * part + 2, :, :, :]
            else:
                src = src[:, :, 256 * part : 256 * part + 256].rearrange("p t n -> p n t")
            copy(out=dst, in_=src)

        def quantise_w(m):
            nc.vector.quantize_mx(
                out=w_codes[m][:].bitcast(FP8X4),
                scales=w_scales[m],
                in_=w_grouped[m][:].rearrange("p n t -> p (n t)"),
            )

        def multiply(dst, lhs, lhs_scale, rhs, rhs_scale, start=True, stop=True):
            nc.tensor.matmul_mx(
                out=dst,
                lhsT=lhs.bitcast(FP8X4),
                lhsT_scale=lhs_scale,
                rhs=rhs.bitcast(FP8X4),
                rhs_scale=rhs_scale,
                start=start,
                stop=stop,
            )

        pooled = [sb([P, 4, 16], F32, "pooled%d" % m) for m in range(2)]

        def pool_products(m, part):
            ps = bank("pool%d_%d" % (m, part))
            banks["pool", m, part] = ps
            cols = slice(512 * part, 512 * part + 512)
            for k in range(4):
                group = slice(P * k, P * k + P)
                multiply(
                    ps[:],
                    w_codes[m][:, group],
                    w_scales[m][:, group],
                    u_codes[m][:, cols],
                    u_scales[m][:, cols],
                    k == 0,
                    k == 3,
                )

        def pool_reduce(m, part):
            ps = banks["pool", m, part]
            if m == 1:
                dst = pooled[1][:, 2 * part : 2 * part + 2, :]
                src = ps[:].rearrange("p (q k y) -> p q k y", q=2, y=R)
            elif part == 0:
                dst = pooled[0][:, :, 0:8]
                src = ps[:].rearrange("p (q k y) -> p q k y", q=4, y=R)
            else:
                dst = pooled[0][:].rearrange("p q (n k l) -> p n k q l", n=2, l=2)[:, 1, :, :, :]
                src = ps[:].rearrange("p (k q l y) -> p k q l y", k=4, q=4, l=2)
            nc.vector.tensor_reduce(out=dst, in_=src, axis=AX, op=ADD)

        pooled2 = sb([P, 2, K], F32, "pooled2")

        def pool2_products(half):
            ps = bank("pool2_%d" % half)
            for k in range(4):
                rows = slice(512 * half + P * k, 512 * half + P * k + P)
                multiply(
                    ps[:],
                    u_codes[2][:, rows],
                    u_scales[2][:, rows],
                    w_codes[2][:, 0:K],
                    w_scales[2][:, 0:K],
                    k == 0,
                    k == 3,
                )
            banks["pool2", half] = ps

        def pool2_copy(half):
            nc.scalar.copy(out=pooled2[:, half, :], in_=banks["pool2", half][:])

        def spread_w(m):
            nc.vector.tensor_copy(
                out=spread_codes[m][:, GAP:].rearrange("p (z c) -> p z c", c=P)[:, :, 0:E].bitcast(I32),
                in_=w_codes[m][:].rearrange("p (z e) -> p z e", e=E).bitcast(I32),
            )
            nc.vector.tensor_copy(
                out=spread_scales[m][1][:, EDGE + E : EDGE + E + K].bitcast(I32),
                in_=spread_scales[m][0][:, EDGE : EDGE + K].bitcast(I32),
            )

        y0_half0 = sb([P, R, 8, R], F32, "y0_half0")
        y1 = [sb([P, 4, R, 8, 4], F32, "y1_%d" % half) for half in range(2)]
        y0_half1 = sb([P, 4, R, 32], F32, "y0_half1")

        def y_place(m, half, z):
            if m == 0:
                return y0_half0[:, z, :, :].rearrange("p k (b a) -> p k b a", b=4)
            return y1[half][:, :, z, :, :].rearrange("p b k a -> p k b a")

        def bias_of(m, z):
            i = 4 * (z % 4) + z // 4 if m == 0 else R + z
            return vec[:, i : i + 1]

        def add_bias(m, half, z, ps):
            nc.scalar.activation(
                out=y_place(m, half, z),
                in_=ps.rearrange("p (k b a) -> p k b a", k=8, b=4),
                func=IDENTITY,
                bias=bias_of(m, z),
            )

        def masked_passes(dst, m, z, columns):
            for q in range(4):
                shift = (z - q) % 2
                code = GAP + P * z - E * q
                scale_col = EDGE + E * (z - q + shift)
                cols = columns(q)
                multiply(
                    dst,
                    spread_codes[m][:, code : code + P],
                    spread_scales[m][shift][:, scale_col : scale_col + P],
                    u_codes[m][:, cols],
                    u_scales[m][:, cols],
                    q == 0,
                    q == 3,
                )

        def quadrant_product(k):
            ps = bank("quadrant%d" % k)
            banks["quadrant", k] = ps
            rows = slice(512 + P * k, 512 + P * k + P)
            multiply(ps[:], u_codes[0][:, rows], u_scales[0][:, rows], w_codes[0][:, 0:K], w_scales[0][:, 0:K])

        def quadrant_turn(k):
            nc.vector.transpose(out=y0_half1[:, k, :, :].rearrange("p z r -> p (z r)"), in_=banks["quadrant", k][:])

        def quadrant_bias(k):
            nc.vector.tensor_tensor(
                out=y0_half1[:, k, :, :].rearrange("p (a b) r -> p a b r", a=4),
                in0=y0_half1[:, k, :, :].rearrange("p (a b) r -> p a b r", a=4),
                in1=vec[:, 0:R].rearrange("p (b a) -> p a b", b=4).unsqueeze(3).to_broadcast([P, 4, 4, 32]),
                op=ADD,
            )

        def masked(m, half, k):
            ps = bank("masked%d_%d_%d" % (m, half, k))
            banks["masked", m, half, k] = ps

            def columns(q):
                start = 256 * q + P * half if m == 1 else P * q
                return slice(start, start + P)

            for d in range(4):
                masked_passes(ps[:, P * d : P * d + P], m, 4 * k + d, columns)

        def masked_out(m, half, k):
            for d in range(4):
                add_bias(m, half, 4 * k + d, banks["masked", m, half, k][:, P * d : P * d + P])

        def masked_both_halves(k):
            ps = bank("masked_both%d" % k)
            for d in range(2):
                masked_passes(ps[:, 256 * d : 256 * d + 256], 1, 2 * k + d, lambda q: slice(256 * q, 256 * q + 256))
            for half in range(2):
                for d in range(2):
                    start = 256 * d + P * half
                    add_bias(1, half, 2 * k + d, ps[:, start : start + P])

        b_mean = sb([P, 1], F32, "b_mean")
        b_pool = sb([P, 4], F32, "b_pool")

        def mean_bias():
            nc.vector.tensor_reduce(out=b_mean[:], in_=vec[:, 0:32], axis=AX, op=ADD)
            nc.vector.scalar_tensor_tensor(
                out=b_pool[:],
                in0=b_mean[:].to_broadcast([P, 4]),
                scalar=1.0 / R,
                in1=vec[:, 32:36],
                op0=MULT,
                op1=ADD,
            )

        wp_wide = sb([P, 4, K], BF16, "wp_wide")

        def widen_wp(t):
            nc.scalar.activation(
                out=wp_wide[:, t, :], in_=wp_in[:, t, :].bitcast(E4M3), func=COPY, scale=wp_row_scale[:, t : t + 1]
            )

        weight = sb([P, 3, 16], F32, "weight")
        weight_b2 = sb([P, 4, 4], F32, "weight_b2")
        step_tile = {}

        def pool2_finish():
            ps = bank("pool2_ps")
            for c in range(4):
                for half in range(2):
                    k = 4 * c + 2 * half
                    nc.tensor.matmul(
                        ps[:, k : k + 2],
                        lhsT=pooled2[:, half, P * c : P * c + P],
                        rhs=in_image[:],
                        start=True,
                        stop=True,
                    )
            part2 = sb([P, 4, 4], F32, "part2")
            nc.vector.tensor_tensor(
                out=part2[:],
                in0=ps[:, 0:16].rearrange("p (c n) -> p c n", c=4),
                in1=b_pool[:].unsqueeze(2).to_broadcast([P, 4, 4]),
                op=ADD,
            )
            step_tile["part2"] = part2

        def pool01_finish():
            ps = bank("pool01_ps")
            for m in range(2):
                nc.tensor.matmul(
                    ps[:, 0:64],
                    lhsT=sum_e[:],
                    rhs=pooled[m][:].rearrange("p q k -> p (q k)"),
                    start=(m == 0),
                    stop=(m == 1),
                )
            picked = sb([P, 4, 16], F32, "picked")
            nc.vector.tensor_tensor(
                out=picked[:],
                in0=ps[:, 0:64].rearrange("p (q k) -> p q k", q=4),
                in1=in_quadrant[:].unsqueeze(2).to_broadcast([P, 4, 16]),
                op=MULT,
            )
            part01 = sb([P, 16], F32, "part01")
            nc.vector.tensor_reduce(out=part01[:], in_=picked[:].rearrange("p q k -> p k q"), axis=AX, op=ADD)
            step_tile["part01"] = part01

        def softmax(step):
            if step == 0:
                pool = sb([P, 4, 4], F32, "pool")
                part01 = step_tile["part01"][:].rearrange("p (n f h l) -> p n f h l", n=2, f=2, h=2)
                part2 = step_tile["part2"][:].rearrange("p (h f) (n l) -> p n f h l", h=2, n=2)
                for half in range(2):
                    nc.vector.tensor_tensor(
                        out=pool[:].rearrange("p (h f) (n l) -> p n f h l", h=2, n=2)[:, half, :, :, :],
                        in0=part01[:, half, :, :, :],
                        in1=part2[:, half, :, :, :],
                        op=ADD,
                    )
                step_tile["pool"] = pool
            elif step == 1:
                logit = sb([P, 3, 16], F32, "logit")
                nc.vector.tensor_tensor(
                    out=logit[:].rearrange("p m (c n) -> p m c n", c=4),
                    in0=step_tile["pool"][:].unsqueeze(1).to_broadcast([P, 3, 4, 4]),
                    in1=vec[:, 36:48].rearrange("p (m c) -> p m c", m=3).unsqueeze(3).to_broadcast([P, 3, 4, 4]),
                    op=MULT,
                )
                step_tile["logit"] = logit
            elif step == 2:
                largest = sb([P, 16], F32, "largest")
                nc.vector.tensor_reduce(
                    out=largest[:], in_=step_tile["logit"][:].rearrange("p m k -> p k m"), axis=AX, op=MAX
                )
                step_tile["largest"] = largest
            elif step == 3:
                shifted = sb([P, 3, 16], F32, "shifted")
                nc.vector.tensor_tensor(
                    out=shifted[:],
                    in0=step_tile["logit"][:],
                    in1=step_tile["largest"][:].unsqueeze(1).to_broadcast([P, 3, 16]),
                    op=SUB,
                )
                expo = sb([P, 3, 16], F32, "expo")
                nc.scalar.activation(out=expo[:], in_=shifted[:], func=EXP)
                step_tile["expo"] = expo
            elif step == 4:
                total = sb([P, 16], F32, "total")
                nc.vector.tensor_reduce(
                    out=total[:], in_=step_tile["expo"][:].rearrange("p m k -> p k m"), axis=AX, op=ADD
                )
                expo_gp = sb([P, 3, 4, 4], F32, "expo_gp")
                nc.vector.tensor_tensor(
                    out=expo_gp[:],
                    in0=step_tile["expo"][:].rearrange("p m (c n) -> p m c n", c=4),
                    in1=vec[:, 48:52].unsqueeze(1).unsqueeze(3).to_broadcast([P, 3, 4, 4]),
                    op=MULT,
                )
                step_tile["total"], step_tile["expo_gp"] = total, expo_gp
            elif step == 5:
                inverse = sb([P, 16], F32, "inverse")
                nc.vector.reciprocal(out=inverse[:], in_=step_tile["total"][:])
                step_tile["inverse"] = inverse
            elif step == 6:
                nc.vector.tensor_tensor(
                    out=weight[:],
                    in0=step_tile["expo_gp"][:].rearrange("p m c n -> p m (c n)"),
                    in1=step_tile["inverse"][:].unsqueeze(1).to_broadcast([P, 3, 16]),
                    op=MULT,
                )
            else:
                nc.vector.tensor_tensor(
                    out=weight_b2[:],
                    in0=weight[:, 2, :].rearrange("p (c n) -> p c n", c=4),
                    in1=vec[:, 32:36].unsqueeze(2).to_broadcast([P, 4, 4]),
                    op=MULT,
                )

        f_sum = keep.tile([P, 4, 4, PIXELS], BF16, name="f_sum", tag="u0", align_bytes=64)
        partial = {}

        def branch2(half, c):
            ps = bank("y2_%d_%d" % (half, c))
            banks["y2", half, c] = ps
            chunk = slice(P * c, P * c + P)
            cols = slice(512 * half, 512 * half + 512)
            multiply(ps[:], w_codes[2][:, chunk], w_scales[2][:, chunk], u_codes[2][:, cols], u_scales[2][:, cols])

        def weigh2(half, c):
            view = banks["y2", half, c][:].rearrange("p (b l a j) -> p l a b j", b=4, l=2, a=4)
            for l in range(2):
                n = 2 * half + l
                k = 4 * c + n
                part = work.tile([P, R, R], F32, name="part", bufs=16)
                partial[c, n] = part
                nc.scalar.activation(
                    out=part[:].rearrange("p (a b) j -> p a b j", a=4),
                    in_=view[:, l, :, :, :],
                    func=IDENTITY,
                    scale=weight[:, 2, k : k + 1],
                    bias=weight_b2[:, c, n : n + 1],
                )

        def weigh01(n, chunks, part=None):
            half, l = n // 2, n % 2
            a = slice(0, 4) if part is None else slice(2 * part, 2 * part + 2)
            rows = slice(4 * a.start, 4 * a.stop)
            for c in chunks:
                k = 4 * c + n
                group = 2 * (c % 2) + c // 2
                if half == 0:
                    y0 = y0_half0[:, rows, 2 * group + l, :]
                else:
                    y0 = y0_half1[:, group, rows, R * l : R * l + R]
                nc.vector.scalar_tensor_tensor(
                    out=partial[c, n][:, rows, :],
                    in0=y0,
                    scalar=weight[:, 0, k : k + 1],
                    in1=partial[c, n][:, rows, :],
                    op0=MULT,
                    op1=ADD,
                )
            for c in chunks:
                k = 4 * c + n
                group = 2 * (c % 2) + c // 2
                so_far = partial[c, n][:].rearrange("p i j -> p (i j)")
                nc.vector.scalar_tensor_tensor(
                    out=f_sum[:, c, n, :].rearrange("p (a r) -> p r a", a=4)[:, :, a],
                    in0=y1[half][:, :, :, 2 * group + l, a].rearrange("p b j a -> p (b j) a"),
                    scalar=weight[:, 1, k : k + 1],
                    in1=so_far.rearrange("p (a r) -> p r a", a=4)[:, :, a],
                    op0=MULT,
                    op1=ADD,
                )

        f_rows, f_grouped, f_quantised = {}, {}, {}

        def f_to_tokens(n, part):
            ps = bank("f_rows%d_%d" % (n, part), BF16, 512)
            for c in range(4):
                nc.tensor.transpose(
                    ps[:, P * c : P * c + P], f_sum[:, c, n, P * part : P * part + P], ident_bf[:]
                )
            rows = work.tile([P, K], BF16, name="rows")
            nc.scalar.copy(out=rows[:], in_=ps[:])
            f_rows[n, part] = rows

        def f_to_channels(n, part):
            ps = bank("f_words%d_%d" % (n, part), F32, 256)
            words = f_rows[n, part][:].bitcast(F32)
            for v in range(2):
                nc.tensor.transpose(ps[:, P * v : P * v + P], words[:, v::2], perm_f[:])
            if n not in f_grouped:
                grouped = work.tile([P, 4 * PIXELS], BF16, name="grouped", align_bytes=64)
                f_grouped[n] = grouped
            nc.scalar.copy(
                out=f_grouped[n][:].bitcast(F32).rearrange("p (b g c v) -> p g b c v", b=4, g=2, v=2)[:, part, :, :, :],
                in_=ps[:].rearrange("p (v b c) -> p b c v", v=2, b=4),
            )

        def quantise_f(n):
            codes = work.tile([P, PIXELS], U32, name="codes", align_bytes=64)
            scales = work.tile([P, PIXELS], U8, name="scales", align_bytes=64)
            nc.vector.quantize_mx(out=codes[:].bitcast(FP8X4), scales=scales[:], in_=f_grouped[n][:])
            f_quantised[n] = (codes, scales)

        def project(n, part, copy):
            codes, scales = f_quantised[n]
            rows = slice(P * part, P * part + P)
            ps = bank("project%d_%d" % (n, part))
            multiply(ps[:], codes[:, rows], scales[:, rows], w_codes[3][:, 0:K], w_scales[3][:, 0:K])
            result = work.tile([P, K], F32, name="result", bufs=4)
            copy(out=result[:], in_=ps[:])
            nc.sync.dma_start(out=out[n].rearrange("i j c -> (i j) c")[rows, :], in_=result[:])

        with tc.manual_schedule():
            for k in (1, 3, 0, 2):
                scale(1, k, 0)
            for k in (1, 3):
                scale(1, k, 1)
            turn(1, 3)
            scale(1, 2, 1)
            for k in (2, 1):
                turn(1, k)
            interleave_w(1, 1, nc.vector.tensor_copy)
            scale(1, 0, 1)
            turn(1, 0)
            collect(1, 2)
            interleave_w(1, 0, nc.vector.tensor_copy)
            collect(1, 1)
            for k in range(2):
                scale(2, k)
            collect(1, 3)
            scale(2, 2)
            quantise_w(1)
            scale(2, 3)
            quantise_u(1, 1)
            spread_w(1)
            turn(2, 0)
            small_vectors()
            turn(2, 2)
            for k in (0, 3):
                scale(0, k)
            turn(2, 1)
            collect(2, 2)
            turn(2, 3)
            for k in (2, 1):
                collect(k, 0)
            collect(2, 1)
            pool_products(1, 1)
            collect(2, 3)
            turn(0, 0)
            for k in (2, 1):
                scale(0, k)
            turn(0, 3)
            quantise_u(1, 0)
            for k in (2, 1):
                turn(0, k)
            interleave_w(2, 0, nc.scalar.copy)
            pool_reduce(1, 1)
            collect(0, 3)
            interleave_w(0, 1, nc.vector.tensor_copy)
            masked(1, 0, 2)
            interleave_w(2, 1, nc.scalar.copy)
            interleave_w(0, 0, nc.vector.tensor_copy)
            quantise_w(2)
            for k in range(2):
                quantise_u(2, k)
            collect(0, 2)
            widen_wp(3)
            for k in (1, 0):
                collect(0, k)
            masked_both_halves(2)
            quantise_w(0)
            masked_both_halves(3)
            pool_products(1, 0)
            masked_out(1, 0, 2)
            quantise_u(0, 1)
            spread_w(0)
            pool_reduce(1, 0)
            masked(1, 0, 3)
            masked_out(1, 0, 3)
            quadrant_product(2)
            pool2_products(1)
            quantise_u(0, 0)
            pool_products(0, 1)
            widen_wp(2)
            masked_both_halves(1)
            pool_reduce(0, 1)
            pool_products(0, 0)
            widen_wp(0)
            masked(0, 0, 2)
            pool_reduce(0, 0)
            quadrant_product(3)
            mean_bias()
            quadrant_turn(2)
            pool2_products(0)
            pool2_copy(1)
            quadrant_product(1)
            widen_wp(1)
            branch2(1, 1)
            pool2_copy(0)
            pool01_finish()
            quadrant_turn(3)
            pool2_finish()
            softmax(0)
            interleave_w(3, 0, nc.scalar.copy)
            softmax(1)
            masked_out(0, 0, 2)
            softmax(2)
            interleave_w(3, 1, nc.scalar.copy)
            masked(0, 0, 3)
            quadrant_product(0)
            masked_out(0, 0, 3)
            softmax(3)
            quadrant_turn(1)
            branch2(0, 0)
            softmax(4)
            for k in range(2):
                masked(0, 0, k)
            quadrant_bias(1)
            masked_out(0, 0, 0)
            for k in range(5, 8):
                softmax(k)
            weigh2(1, 1)
            branch2(0, 1)
            quadrant_turn(0)
            weigh2(0, 0)
            masked_out(0, 0, 1)
            weigh2(0, 1)
            masked_both_halves(0)
            branch2(0, 3)
            branch2(1, 0)
            for k in (3, 2):
                quadrant_bias(k)
            branch2(0, 2)
            for k in (3, 2):
                weigh2(0, k)
            quadrant_bias(0)
            branch2(1, 3)
            quantise_w(3)
            branch2(1, 2)
            weigh01(0, (0, 1))
            masked(1, 1, 2)
            weigh2(1, 2)
            masked(1, 1, 3)
            weigh01(1, (0, 1))
            weigh01(0, (2, 3))
            weigh2(1, 0)
            masked_out(1, 1, 2)
            weigh2(1, 3)
            masked_out(1, 1, 3)
            f_to_tokens(0, 0)
            weigh01(1, (2, 3))
            for k in range(2):
                f_to_tokens(k, 1)
            weigh01(2, (0, 1))
            f_to_tokens(1, 0)
            for k in range(2):
                f_to_channels(0, k)
            for k in (1, 0):
                f_to_channels(1, k)
            weigh01(2, (2, 3))
            quantise_f(0)
            for k in range(2):
                f_to_tokens(2, k)
            quantise_f(1)
            for k in range(2):
                project(k, 0, nc.scalar.copy)
            f_to_channels(2, 1)
            for k in (1, 0):
                project(k, 1, nc.scalar.copy)
            weigh01(3, (0, 1, 2, 3), 0)
            f_to_channels(2, 0)
            f_to_tokens(3, 0)
            weigh01(3, (0, 1, 2, 3), 1)
            f_to_tokens(3, 1)
            f_to_channels(3, 0)
            quantise_f(2)
            f_to_channels(3, 1)
            project(2, 0, nc.scalar.copy)
            quantise_f(3)
            project(2, 1, nc.scalar.copy)
            project(3, 1, nc.vector.tensor_copy)
            project(3, 0, nc.scalar.copy)
